import numpy as np
import ml_dtypes


def mxq(x, axis, fmt="e4m3"):
    dtype, down = {"e4m3": (ml_dtypes.float8_e4m3fn, 7), "e5m2": (ml_dtypes.float8_e5m2, 14)}[fmt]
    v = np.moveaxis(np.asarray(x, np.float32).astype(ml_dtypes.bfloat16).astype(np.float64), axis, -1)
    blocks = v.reshape(v.shape[:-1] + (-1, 32))
    amax = np.abs(blocks).max(-1, keepdims=True)
    byte = np.maximum(np.where(amax > 0, np.frexp(amax)[1] - 1 + 127, 0) - down, 1)
    scale = np.exp2(byte - 127.0)
    codes = (blocks / scale).astype(np.float32).astype(dtype).astype(np.float64)
    return np.moveaxis((codes * scale).reshape(v.shape), -1, axis)


WIDE = False


def mx_kscale(k):
    if not WIDE:
        return np.ones(k)
    levels = np.array([10, -10, 5, -5, 0])
    if k % 512:
        return np.exp2(np.random.permutation(np.resize(levels, k // 32))).repeat(32)
    a = np.empty((k // 512, 16))
    for p in range(k // 512):
        a[p, :8] = np.random.permutation(np.resize(levels, 8))
        for g in range(8):
            far = levels[np.abs(levels - a[p, g]) >= 10]
            a[p, g + 8] = far[np.random.randint(len(far))]
    return np.exp2(a.ravel()).repeat(32)


BF16 = ml_dtypes.bfloat16


def bf(x):
    return np.asarray(x, np.float32).astype(BF16)


def f64(x):
    return np.asarray(x).astype(np.float64)


E2M1 = np.array([0.0, 0.5, 1.0, 1.5, 2.0, 3.0, 4.0, 6.0, -0.0, -0.5, -1.0, -1.5, -2.0, -3.0, -4.0, -6.0])


def pack_weight(w, fmt):
    k, n = w.shape
    w = f64(bf(w)).reshape(k // 32, 32, n)
    amax = np.abs(w).max(1)
    if fmt == "e4m3":
        byte = np.frexp(amax)[1] - 1 + 127 - 7
    else:
        mant, ex = np.frexp(amax / 6.0)
        byte = np.where(mant > 0.5, ex, ex - 1) + 127
    byte = np.clip(np.where(amax > 0, byte, 1), 1, 254)
    scaled = (w * np.exp2(127.0 - byte)[:, None, :]).reshape(k, n).astype(np.float32)
    by_word = np.ascontiguousarray(scaled.reshape(k // 512, 128, 4, n).transpose(0, 1, 3, 2))
    if fmt == "e4m3":
        words = by_word.astype(ml_dtypes.float8_e4m3fn).view(np.uint8)
    else:
        c = by_word.astype(ml_dtypes.float4_e2m1fn).view(np.uint8) & 0xF
        words = c[..., 0::2] | (c[..., 1::2] << 4)
    return np.ascontiguousarray(words), np.ascontiguousarray(byte.astype(np.uint8).reshape(k // 512, 16, n))


def unpack_weight(words, scales, fmt):
    g, p, n, _ = words.shape
    if fmt == "e4m3":
        vals = np.ascontiguousarray(words).view(ml_dtypes.float8_e4m3fn).astype(np.float64)
    else:
        nib = np.empty((g, p, n, 4), np.uint8)
        nib[..., 0::2] = words & 0xF
        nib[..., 1::2] = words >> 4
        vals = E2M1[nib]
    vals = vals * np.repeat(np.exp2(scales.astype(np.float64) - 127.0), 8, axis=1)[..., None]
    return vals.transpose(0, 1, 3, 2).reshape(g * 512, n)

def planes(Y):
    n, m = Y.shape
    b = f64(bf(Y)).reshape(n // 32, 32, m)
    amax = np.abs(b).max(1)
    byte = np.clip(np.where(amax > 0, np.frexp(amax)[1] - 1 + 127 - 7, 1), 1, 254)
    codes = (b * np.exp2(127.0 - byte)[:, None, :]).reshape(n, m).astype(np.float32).astype(ml_dtypes.float8_e4m3fn).view(np.uint8)
    words = codes.reshape(n // 512, 128, 4, m).transpose(0, 1, 3, 2)
    return np.ascontiguousarray(words), np.ascontiguousarray(byte.astype(np.uint8).reshape(n // 512, 16, m))


R, N, D, H, O = 8, 128, 512, 1024, 512


def silu_slope(a):
    s = 1.0 / (1.0 + np.exp(-a))
    return s * (1.0 + a * (1.0 - s))


def setup_inputs():
    s, t = mx_kscale(D), mx_kscale(H)
    common = np.random.standard_normal((R, 1, D))
    x = 0.8 * common + 0.6 * np.random.standard_normal((R, N, D))
    gin = 1.0 + 0.2 * np.random.standard_normal(D)
    w1 = np.random.standard_normal((D, H)) / np.sqrt(D)
    b1 = 0.5 * np.random.standard_normal(H)
    gamma = 1.0 + 0.1 * np.random.standard_normal(H)
    w2 = np.random.standard_normal((H, O)) * 0.4 * np.sqrt(D / H)
    beta = np.random.uniform(1.5, 3.0, R)
    w2_words, w2_scales = pack_weight(w2 / t[:, None], "e4m3")
    return {"x": bf(x), "gin": bf(gin * s), "w1": bf(w1 / s[:, None]), "b1": bf(b1),
            "gamma": bf(gamma * t), "w2_words": w2_words, "w2_scales": w2_scales, "beta": bf(beta)}


def core(x, gin, w1, b1, gamma, w2_words, w2_scales, beta):
    x, gin, w1, b1 = f64(x), f64(gin), f64(w1), f64(b1)
    gamma, beta = f64(gamma), f64(beta)
    a = (mxq(x * gin, 2, "e4m3") @ mxq(w1, 0, "e4m3")) + b1
    dphi = silu_slope(a)
    mbar = np.mean(dphi, axis=1)
    p = w1[None, :, :] * mbar[:, None, :] * gamma[None, None, :]
    k = mxq(p, 2, "e4m3") @ unpack_weight(w2_words, w2_scales, "e4m3")
    return beta[:, None, None] * gin[None, :, None] * k


def reference(x, gin, w1, b1, gamma, w2_words, w2_scales, beta):
    R_out = core(x, gin, w1, b1, gamma, w2_words, w2_scales, beta)
    words, scales = planes(np.moveaxis(R_out, 2, 0).reshape(512, -1))
    return R_out, words, scales

@@ -1,0 +1,697 @@
+from contextlib import ExitStack
+
+import concourse.mybir as mybir
+from concourse.masks import make_identity
+
+R, N, D, H, O = 8, 128, 512, 1024, 512
+FLOPS = 2 * R * N * D * H + 2 * R * D * H * O
+
+F32 = mybir.dt.float32
+BF16 = mybir.dt.bfloat16
+U32 = mybir.dt.uint32
+I32 = mybir.dt.int32
+U8 = mybir.dt.uint8
+FP8X4 = mybir.dt.float8_e4m3fn_x4
+ALU = mybir.AluOpType
+ACT = mybir.ActivationFunctionType
+
+P = 128
+PACK = 4
+K_PASS = P * PACK
+G = H // K_PASS
+PAIRS = R // 2
+
+
+def tile_linearrelationmeanjacobian_x2_kernel(
+    tc, x, gin, w1, b1, gamma, w2_words, w2_scales, beta, out_0, out_1, out_2
+):
+    nc = tc.nc
+    with ExitStack() as ctx:
+        keep = ctx.enter_context(tc.tile_pool(name="keep", bufs=1))
+        work = ctx.enter_context(tc.tile_pool(name="work", bufs=2))
+        psum = ctx.enter_context(tc.psum_pool(name="psum", bufs=2))
+        ctx.enter_context(tc.manual_schedule())
+
+        ident_f32 = keep.tile([P, P], F32, name="ident_f32")
+        ident_bf = keep.tile([P, P], BF16, name="ident_bf")
+        gin_bf = keep.tile([P, PACK], BF16, name="gin_bf")
+        b1_bf = keep.tile([P, G, PACK], BF16, name="b1_bf")
+        gamma_bf = keep.tile([P, G, PACK], BF16, name="gamma_bf")
+        beta_bf = keep.tile([P, R], BF16, name="beta_bf")
+        b1_half = keep.tile([P, G, PACK], F32, name="b1_half")
+        b1_full = keep.tile([P, G, PACK], F32, name="b1_full")
+        gamma_n = keep.tile([P, G, PACK], F32, name="gamma_n")
+        out_gain = keep.tile([P, R, PACK], F32, name="out_gain")
+        warm = keep.tile([P, 1], F32, name="warm")
+        warm_out = keep.tile([P, 1], F32, name="warm_out")
+        x_raw = [keep.tile([P, 2, D], BF16, name="x_raw%d" % q) for q in range(PAIRS)]
+        w1_raw = [keep.tile([P, PACK, K_PASS], BF16, name="w1_raw%d" % g) for g in range(G)]
+        w1_grouped = [keep.tile([P, PACK, P, PACK], BF16, name="w1_grouped%d" % g, align_bytes=64) for g in range(G)]
+        w1_codes = [keep.tile([P, K_PASS], U32, name="w1_codes%d" % g, align_bytes=64) for g in range(G)]
+        w1_scales = [keep.tile([P, K_PASS], U8, name="w1_scales%d" % g, align_bytes=64) for g in range(G)]
+        w1_t = [keep.tile([P, PACK, D], BF16, name="w1_t%d" % g) for g in range(G)]
+        w2_codes = keep.tile([P, G, O], U32, name="w2_codes", align_bytes=64)
+        w2_plane = keep.tile([P, G, O], U8, name="w2_plane", align_bytes=64)
+        x_codes = [keep.tile([P, 2 * N], U32, name="x_codes%d" % q, align_bytes=64) for q in range(PAIRS)]
+        x_scales = [keep.tile([P, 2 * N], U8, name="x_scales%d" % q, align_bytes=64) for q in range(PAIRS)]
+        tanh_sum = keep.tile([P, PAIRS, G, PACK, 2], F32, name="tanh_sum")
+        prod_sum = keep.tile([P, PAIRS, G, PACK, 2], F32, name="prod_sum")
+        slope_sum = keep.tile([P, PAIRS, G, PACK, 2], F32, name="slope_sum")
+        out_plane = keep.tile([P, R * D], U8, name="out_plane", align_bytes=64)
+        live = {}
+
+        def loads():
+            nc.sync.dma_start(out=x_raw[0][:], in_=x[0:2].rearrange("r n d -> n r d"))
+            nc.scalar.dma_start(out=gin_bf[:], in_=gin.rearrange("(p t) -> p t", t=PACK))
+            for g in range(G):
+                cols = w1[:, g * K_PASS : (g + 1) * K_PASS]
+                nc.sync.dma_start(out=w1_raw[g][:], in_=cols.rearrange("(p j) h -> p j h", j=PACK))
+            nc.scalar.dma_start(out=b1_bf[:], in_=b1.rearrange("(g p t) -> p g t", g=G, t=PACK))
+            nc.scalar.dma_start(out=gamma_bf[:], in_=gamma.rearrange("(g p t) -> p g t", g=G, t=PACK))
+            nc.scalar.dma_start(out=beta_bf[:], in_=beta.partition_broadcast(P))
+            for q in range(1, PAIRS):
+                nc.sync.dma_start(out=x_raw[q][:], in_=x[2 * q : 2 * q + 2].rearrange("r n d -> n r d"))
+            nc.sync.dma_start(
+                out=w2_codes[:].bitcast(I32),
+                in_=w2_words.rearrange("g p n t -> p g (n t)").bitcast(I32),
+            )
+            for quad in range(4):
+                nc.sync.dma_start(
+                    out=w2_plane[32 * quad : 32 * quad + 4].bitcast(I32),
+                    in_=w2_scales[:, 4 * quad : 4 * quad + 4, :].rearrange("g q n -> q g n").bitcast(I32),
+                )
+
+        def consts():
+            make_identity(nc, ident_f32[:])
+            make_identity(nc, ident_bf[:])
+            nc.gpsimd.memset(w2_plane[:].bitcast(I32), 0)
+            nc.vector.memset(warm[:], 0.0)
+            nc.scalar.activation(out=warm_out[:], in_=warm[:], func=ACT.Silu)
+
+        def small_act():
+            nc.scalar.activation(out=b1_half[:], in_=b1_bf[:], func=ACT.Copy, scale=0.5)
+            nc.scalar.activation(out=b1_full[:], in_=b1_bf[:], func=ACT.Copy)
+            nc.scalar.activation(out=gamma_n[:], in_=gamma_bf[:], func=ACT.Copy, scale=0.5 / N)
+
+        def small_dve():
+            nc.vector.tensor_tensor(
+                out=out_gain[:],
+                in0=beta_bf[:].unsqueeze(2).to_broadcast([P, R, PACK]),
+                in1=gin_bf[:].unsqueeze(1).to_broadcast([P, R, PACK]),
+                op=ALU.mult,
+            )
+
+        def x_turn(q):
+            bank = psum.tile([P, 2, 2, N], F32, name="x_bank", tag="turn")
+            words = x_raw[q][:].bitcast(F32)
+            for i in range(2):
+                for u in range(2):
+                    nc.tensor.transpose(bank[:, u, i, :], words[:, i, u : D // 2 : 2], ident_f32[:])
+            live["x_bank", q] = bank
+
+        def x_gain(q):
+            bank = live["x_bank", q]
+            xg = work.tile([P, 2 * N, 2, 2], BF16, name="xg", align_bytes=64)
+            src = bank[:].rearrange("p u i n -> p (u i n)").bitcast(BF16)
+            nc.vector.tensor_tensor(
+                out=xg[:],
+                in0=src.rearrange("p (u m e) -> p m u e", u=2, e=2),
+                in1=gin_bf[:].rearrange("p (u e) -> p u e", u=2).unsqueeze(1).to_broadcast([P, 2 * N, 2, 2]),
+                op=ALU.mult,
+            )
+            live["xg", q] = xg
+
+        def x_quant(q):
+            nc.vector.quantize_mx(
+                out=x_codes[q][:].bitcast(FP8X4),
+                scales=x_scales[q][:],
+                in_=live["xg", q][:].rearrange("p m u e -> p (m u e)"),
+            )
+
+        def w1_group(g, t0, t1, on_scalar):
+            src = w1_raw[g][:].rearrange("p j (m t) -> p t m j", t=PACK)[:, t0:t1]
+            if on_scalar:
+                nc.scalar.copy(out=w1_grouped[g][:, t0:t1], in_=src)
+            else:
+                nc.vector.tensor_copy(out=w1_grouped[g][:, t0:t1], in_=src)
+
+        def w1_quant(g, t0, t1):
+            nc.vector.quantize_mx(
+                out=w1_codes[g][:, t0 * P : t1 * P].bitcast(FP8X4),
+                scales=w1_scales[g][:, t0 * P : t1 * P],
+                in_=w1_grouped[g][:, t0:t1].rearrange("p t m j -> p (t m j)"),
+            )
+
+        def w1_turn(g, half):
+            bank = psum.tile([P, 2, PACK, P], BF16, name="w1_bank", tag="weave")
+            for tl in range(2):
+                for j in range(PACK):
+                    nc.tensor.transpose(bank[:, tl, j, :], w1_raw[g][:, j, 2 * half + tl : K_PASS : PACK], ident_bf[:])
+            live["w1_bank", g, half] = bank
+
+        def w1_out(g, half, on_scalar):
+            src = live["w1_bank", g, half][:].rearrange("p t j c -> p (t j c)")
+            dst = w1_t[g][:, 2 * half : 2 * half + 2].rearrange("p t d -> p (t d)")
+            if on_scalar:
+                nc.scalar.copy(out=dst, in_=src)
+            else:
+                nc.vector.tensor_copy(out=dst, in_=src)
+
+        def pre_mm(q, g, half):
+            bank = psum.tile([P, 2, 2 * N], F32, name="pre_bank", tag="pre")
+            for tl in range(2):
+                cols = slice((2 * half + tl) * P, (2 * half + tl + 1) * P)
+                nc.tensor.matmul_mx(
+                    out=bank[:, tl, :],
+                    lhsT=w1_codes[g][:, cols].bitcast(FP8X4),
+                    lhsT_scale=w1_scales[g][:, cols],
+                    rhs=x_codes[q][:].bitcast(FP8X4),
+                    rhs_scale=x_scales[q][:],
+                    start=True,
+                    stop=True,
+                )
+            live["pre", q, g, half] = bank
+
+        def pre_act(q, g, t):
+            bank = live["pre", q, g, t // 2]
+            silu = work.tile([P, 2, N], F32, name="silu", bufs=4)
+            tanh = work.tile([P, 2, N], F32, name="tanh", bufs=4)
+            for i in range(2):
+                nc.scalar.activation(
+                    out=tanh[:, i, :],
+                    in_=bank[:, t % 2, i * N : (i + 1) * N],
+                    func=ACT.Tanh,
+                    bias=b1_half[:, g, t : t + 1],
+                    scale=0.5,
+                    accum_out=tanh_sum[:, q, g, t, i : i + 1],
+                )
+            nc.scalar.activation(
+                out=silu[:].rearrange("p i n -> p (i n)"),
+                in_=bank[:, t % 2, :],
+                func=ACT.Silu,
+                bias=b1_full[:, g, t : t + 1],
+            )
+            live["st", q, g, t] = (silu, tanh)
+
+        def pre_prod(q, g, t):
+            silu, tanh = live["st", q, g, t]
+            prod = work.tile([P, 2, N], F32, name="prod")
+            for i in range(2):
+                nc.vector.scalar_tensor_tensor(
+                    out=prod[:, i, :],
+                    in0=tanh[:, i, :],
+                    scalar=1.0,
+                    in1=silu[:, i, :],
+                    op0=ALU.subtract,
+                    op1=ALU.mult,
+                    accum_out=prod_sum[:, q, g, t, i : i + 1],
+                )
+
+        def slope(q, g):
+            nc.vector.scalar_tensor_tensor(
+                out=slope_sum[:, q, g].rearrange("p t i -> p (t i)"),
+                in0=tanh_sum[:, q, g].rearrange("p t i -> p (t i)"),
+                scalar=float(N),
+                in1=prod_sum[:, q, g].rearrange("p t i -> p (t i)"),
+                op0=ALU.add,
+                op1=ALU.subtract,
+            )
+
+        def p_scale(r, g):
+            rows = work.tile([P, PACK, D], BF16, name="p_rows", bufs=4)
+            for t in range(PACK):
+                nc.vector.tensor_scalar(
+                    out=rows[:, t, :],
+                    in0=w1_t[g][:, t, :],
+                    scalar1=slope_sum[:, r // 2, g, t, r % 2 : r % 2 + 1],
+                    scalar2=gamma_n[:, g, t : t + 1],
+                    op0=ALU.mult,
+                    op1=ALU.mult,
+                )
+            live["rows", r, g] = rows
+
+        def grouped(r, g):
+            if ("grouped", r, g) not in live:
+                live["grouped", r, g] = work.tile([P, D, PACK], BF16, name="p_grouped", bufs=4, align_bytes=64)
+            return live["grouped", r, g]
+
+        def p_weave_dve(r, g, half):
+            cols = slice(half * 256, (half + 1) * 256)
+            nc.vector.tensor_copy(
+                out=grouped(r, g)[:, cols, :].rearrange("p (c i) t -> p c t i", i=4),
+                in_=live["rows", r, g][:, :, cols].rearrange("p t (c i) -> p c t i", i=4),
+            )
+
+        def p_weave_dve_all(r, g):
+            nc.vector.tensor_copy(
+                out=grouped(r, g)[:].rearrange("p (c i) t -> p c t i", i=4),
+                in_=live["rows", r, g][:].rearrange("p t (c i) -> p c t i", i=4),
+            )
+
+        def p_weave_mm(r, g, half):
+            bank = psum.tile([P, 2, P, PACK], BF16, name="weave_bank", tag="weave")
+            for s in range(2):
+                d0 = (2 * half + s) * P
+                nc.tensor.matmul(
+                    bank[:, s].rearrange("p d t -> p (d t)"),
+                    lhsT=ident_bf[:],
+                    rhs=live["rows", r, g][:, :, d0 : d0 + P].rearrange("p t d -> p d t"),
+                    start=True,
+                    stop=True,
+                )
+            live["weave", r, g, half] = bank
+
+        def p_weave_out(r, g, half):
+            nc.scalar.copy(
+                out=grouped(r, g)[:, half * 256 : (half + 1) * 256, :].rearrange("p d t -> p (d t)"),
+                in_=live["weave", r, g, half][:].rearrange("p s d t -> p (s d t)"),
+            )
+
+        def p_quant(r, g):
+            codes = work.tile([P, D], U32, name="p_codes", bufs=6, align_bytes=64)
+            scales = work.tile([P, D], U8, name="p_scales", bufs=6, align_bytes=64)
+            nc.vector.quantize_mx(
+                out=codes[:].bitcast(FP8X4),
+                scales=scales[:],
+                in_=live["grouped", r, g][:].rearrange("p d t -> p (d t)"),
+            )
+            live["p", r, g] = (codes, scales)
+
+        def k_mm(r, j):
+            bank = psum.tile([P, O], F32, name="k_bank", tag="k")
+            cols = slice(j * P, (j + 1) * P)
+            for g in range(G):
+                codes, scales = live["p", r, g]
+                nc.tensor.matmul_mx(
+                    out=bank[:],
+                    lhsT=codes[:, cols].bitcast(FP8X4),
+                    lhsT_scale=scales[:, cols],
+                    rhs=w2_codes[:, g, :].bitcast(FP8X4),
+                    rhs_scale=w2_plane[:, g, :],
+                    start=(g == 0),
+                    stop=(g == G - 1),
+                )
+            live["k", r, j] = bank
+
+        def y_out(r, j, on_scalar):
+            if ("y", r, j // 2) not in live:
+                live["y", r, j // 2] = work.tile([P, 2, O], F32, name="y", bufs=5)
+            y = live["y", r, j // 2]
+            gain = out_gain[:, r, j : j + 1]
+            if on_scalar:
+                nc.scalar.activation(out=y[:, j % 2, :], in_=live["k", r, j][:], func=ACT.Copy, scale=gain)
+            else:
+                nc.vector.tensor_scalar(
+                    out=y[:, j % 2, :], in0=live["k", r, j][:], scalar1=gain, scalar2=None, op0=ALU.mult
+                )
+
+        def y_store(r, half):
+            rows = out_0[r].rearrange("(c j) o -> c j o", j=PACK)
+            nc.sync.dma_start(out=rows[:, 2 * half : 2 * half + 2, :], in_=live["y", r, half][:])
+
+        def y_round(r, half, on_scalar):
+            if ("y_bf", r, half) not in live:
+                live["y_bf", r, half] = work.tile([P, 2, O], BF16, name="y_bf", bufs=3)
+            y_bf = live["y_bf", r, half]
+            if on_scalar:
+                nc.scalar.copy(out=y_bf[:], in_=live["y", r, half][:])
+            else:
+                nc.vector.tensor_copy(out=y_bf[:], in_=live["y", r, half][:])
+
+        def y_turn(r, half):
+            bank = psum.tile([P, 2, 2, P], F32, name="y_bank", tag="turn")
+            words = live["y_bf", r, half][:].bitcast(F32)
+            for jl in range(2):
+                for u in range(2):
+                    nc.tensor.transpose(bank[:, jl, u, :], words[:, jl, u : O // 2 : 2], ident_f32[:])
+            live["y_bank", r, half] = bank
+
+        def y_weave(r, half, on_scalar):
+            if ("y_grouped", r) not in live:
+                live["y_grouped", r] = work.tile([P, P, PACK, 2], F32, name="y_grouped", align_bytes=64)
+            dst = live["y_grouped", r][:, :, 2 * half : 2 * half + 2, :]
+            src = live["y_bank", r, half][:].rearrange("p j u c -> p c j u")
+            if on_scalar:
+                nc.scalar.copy(out=dst, in_=src)
+            else:
+                nc.vector.tensor_copy(out=dst, in_=src)
+
+        def y_quant(r):
+            codes = work.tile([P, D], U32, name="y_codes", bufs=3, align_bytes=64)
+            cols = slice(r * D, (r + 1) * D)
+            nc.vector.quantize_mx(
+                out=codes[:].bitcast(FP8X4),
+                scales=out_plane[:, cols],
+                in_=live["y_grouped", r][:].rearrange("p c j u -> p (c j u)").bitcast(BF16),
+            )
+            nc.sync.dma_start(
+                out=out_1[0, :, cols, :].rearrange("p m t -> p (m t)").bitcast(I32), in_=codes[:].bitcast(I32)
+            )
+
+        def plane_store(r0, r1):
+            cols = slice(r0 * D, r1 * D)
+            for quad in range(4):
+                nc.sync.dma_start(
+                    out=out_2[0, 4 * quad : 4 * quad + 4, cols].bitcast(I32),
+                    in_=out_plane[32 * quad : 32 * quad + 4, cols].bitcast(I32),
+                )
+
+
+        consts()
+        loads()
+        x_turn(0)
+        x_gain(0)
+        x_quant(0)
+        w1_group(0, 0, 2, False)
+        w1_group(1, 2, 4, False)
+        w1_group(0, 2, 4, True)
+        w1_turn(0, 0)
+        w1_turn(0, 1)
+        w1_quant(0, 0, 2)
+        x_turn(1)
+        w1_quant(1, 2, 4)
+        x_gain(1)
+        small_dve()
+        w1_quant(0, 2, 4)
+        x_quant(1)
+        w1_out(0, 0, True)
+        w1_group(1, 0, 2, False)
+        small_act()
+        x_turn(2)
+        x_gain(2)
+        w1_quant(1, 0, 2)
+        x_quant(2)
+        pre_mm(0, 0, 0)
+        pre_mm(0, 0, 1)
+        x_turn(3)
+        w1_out(0, 1, True)
+        pre_act(0, 0, 0)
+        w1_turn(1, 0)
+        pre_act(0, 0, 2)
+        x_gain(3)
+        pre_act(0, 0, 1)
+        pre_mm(0, 1, 0)
+        pre_prod(0, 0, 0)
+        pre_act(0, 0, 3)
+        pre_mm(0, 1, 1)
+        pre_prod(0, 0, 2)
+        pre_act(0, 1, 0)
+        w1_turn(1, 1)
+        w1_out(1, 0, False)
+        pre_prod(0, 0, 1)
+        pre_prod(0, 0, 3)
+        pre_act(0, 1, 2)
+        pre_act(0, 1, 1)
+        x_quant(3)
+        pre_mm(1, 0, 0)
+        pre_prod(0, 1, 0)
+        pre_act(0, 1, 3)
+        pre_mm(1, 0, 1)
+        slope(0, 0)
+        pre_prod(0, 1, 2)
+        pre_act(1, 0, 0)
+        p_scale(0, 0)
+        pre_prod(0, 1, 1)
+        pre_prod(0, 1, 3)
+        pre_act(1, 0, 2)
+        p_weave_dve(0, 0, 0)
+        w1_out(1, 1, True)
+        pre_act(1, 0, 1)
+        pre_mm(1, 1, 0)
+        pre_prod(1, 0, 0)
+        pre_act(1, 0, 3)
+        pre_mm(1, 1, 1)
+        slope(0, 1)
+        pre_prod(1, 0, 2)
+        p_scale(0, 1)
+        pre_act(1, 1, 0)
+        p_scale(1, 0)
+        p_weave_mm(0, 1, 1)
+        pre_prod(1, 0, 1)
+        pre_prod(1, 0, 3)
+        pre_act(1, 1, 2)
+        p_weave_dve(1, 0, 0)
+        pre_act(1, 1, 1)
+        p_weave_mm(0, 1, 0)
+        pre_mm(2, 0, 0)
+        p_weave_out(0, 1, 1)
+        pre_prod(1, 1, 0)
+        pre_act(1, 1, 3)
+        pre_mm(2, 0, 1)
+        slope(1, 0)
+        p_weave_dve(0, 0, 1)
+        pre_prod(1, 1, 2)
+        p_scale(1, 1)
+        pre_act(2, 0, 0)
+        p_scale(2, 0)
+        p_weave_out(0, 1, 0)
+        p_weave_mm(1, 1, 1)
+        pre_prod(1, 1, 1)
+        pre_prod(1, 1, 3)
+        pre_act(2, 0, 2)
+        p_quant(0, 0)
+        p_quant(0, 1)
+        pre_act(2, 0, 1)
+        p_weave_mm(1, 1, 0)
+        pre_mm(2, 1, 0)
+        p_weave_out(1, 1, 1)
+        k_mm(0, 2)
+        pre_prod(2, 0, 0)
+        pre_act(2, 0, 3)
+        pre_mm(2, 1, 1)
+        k_mm(0, 1)
+        slope(1, 1)
+        p_weave_dve(1, 0, 1)
+        p_weave_mm(2, 0, 0)
+        pre_prod(2, 0, 2)
+        p_scale(2, 1)
+        y_out(0, 2, True)
+        pre_act(2, 1, 0)
+        p_scale(3, 0)
+        k_mm(0, 0)
+        p_weave_out(1, 1, 0)
+        p_weave_mm(2, 1, 1)
+        y_out(0, 1, True)
+        pre_prod(2, 0, 1)
+        p_weave_out(2, 0, 0)
+        pre_prod(2, 0, 3)
+        pre_act(2, 1, 2)
+        p_quant(1, 0)
+        y_out(0, 0, True)
+        k_mm(0, 3)
+        y_out(0, 3, True)
+        y_store(0, 0)
+        p_quant(1, 1)
+        pre_act(2, 1, 1)
+        pre_mm(3, 0, 0)
+        p_weave_out(2, 1, 1)
+        k_mm(1, 2)
+        pre_prod(2, 1, 0)
+        pre_act(2, 1, 3)
+        pre_mm(3, 0, 1)
+        p_weave_dve(2, 1, 0)
+        k_mm(1, 1)
+        slope(2, 0)
+        p_weave_dve(2, 0, 1)
+        p_weave_mm(3, 0, 0)
+        pre_prod(2, 1, 2)
+        p_scale(3, 1)
+        y_out(1, 2, True)
+        pre_act(3, 0, 0)
+        p_scale(4, 0)
+        k_mm(1, 0)
+        y_store(0, 1)
+        y_out(1, 1, True)
+        pre_prod(2, 1, 1)
+        p_weave_out(3, 0, 0)
+        pre_prod(2, 1, 3)
+        y_round(0, 0, False)
+        pre_act(3, 0, 2)
+        p_quant(2, 0)
+        y_out(1, 0, True)
+        k_mm(1, 3)
+        y_out(1, 3, True)
+        y_turn(0, 0)
+        y_store(1, 0)
+        p_quant(2, 1)
+        pre_act(3, 0, 1)
+        pre_mm(3, 1, 0)
+        k_mm(2, 2)
+        pre_prod(3, 0, 0)
+        pre_act(3, 0, 3)
+        pre_mm(3, 1, 1)
+        p_weave_dve(3, 1, 0)
+        k_mm(2, 1)
+        slope(2, 1)
+        p_weave_dve(3, 0, 1)
+        y_weave(0, 0, True)
+        y_round(0, 1, False)
+        p_weave_mm(4, 0, 0)
+        pre_prod(3, 0, 2)
+        p_scale(4, 1)
+        y_turn(0, 1)
+        p_weave_dve(3, 1, 1)
+        y_out(2, 2, True)
+        pre_act(3, 1, 0)
+        p_scale(5, 0)
+        k_mm(2, 0)
+        p_weave_mm(4, 1, 1)
+        y_store(1, 1)
+        y_out(2, 1, True)
+        pre_prod(3, 0, 1)
+        p_weave_out(4, 0, 0)
+        pre_prod(3, 0, 3)
+        y_weave(0, 1, True)
+        y_round(1, 0, False)
+        pre_act(3, 1, 2)
+        p_quant(3, 0)
+        y_out(2, 0, True)
+        k_mm(2, 3)
+        y_out(2, 3, True)
+        y_turn(1, 0)
+        y_store(2, 0)
+        p_quant(3, 1)
+        pre_act(3, 1, 1)
+        p_weave_mm(4, 1, 0)
+        p_weave_out(4, 1, 1)
+        k_mm(3, 2)
+        pre_prod(3, 1, 0)
+        pre_act(3, 1, 3)
+        k_mm(3, 1)
+        slope(3, 0)
+        p_weave_dve(4, 0, 1)
+        y_weave(1, 0, True)
+        y_round(1, 1, False)
+        p_weave_mm(5, 0, 0)
+        pre_prod(3, 1, 2)
+        p_scale(5, 1)
+        y_turn(1, 1)
+        y_out(3, 2, True)
+        p_scale(6, 0)
+        k_mm(3, 0)
+        p_weave_out(4, 1, 0)
+        y_store(2, 1)
+        y_out(3, 1, True)
+        pre_prod(3, 1, 1)
+        y_quant(0)
+        p_weave_out(5, 0, 0)
+        pre_prod(3, 1, 3)
+        y_weave(1, 1, True)
+        y_round(2, 0, False)
+        p_quant(4, 0)
+        y_out(3, 0, True)
+        k_mm(3, 3)
+        y_out(3, 3, True)
+        y_turn(2, 0)
+        y_store(3, 0)
+        p_quant(4, 1)
+        p_weave_mm(5, 1, 0)
+        k_mm(4, 2)
+        k_mm(4, 1)
+        slope(3, 1)
+        p_weave_dve(5, 0, 1)
+        y_weave(2, 0, True)
+        y_round(2, 1, False)
+        p_weave_mm(6, 0, 0)
+        p_scale(6, 1)
+        y_turn(2, 1)
+        p_weave_dve(5, 1, 1)
+        y_out(4, 2, True)
+        p_scale(7, 0)
+        k_mm(4, 0)
+        p_weave_out(5, 1, 0)
+        y_store(3, 1)
+        y_out(4, 1, True)
+        y_quant(1)
+        p_weave_out(6, 0, 0)
+        y_weave(2, 1, True)
+        y_round(3, 0, False)
+        p_quant(5, 0)
+        y_out(4, 0, True)
+        k_mm(4, 3)
+        y_out(4, 3, True)
+        y_turn(3, 0)
+        y_store(4, 0)
+        p_quant(5, 1)
+        p_weave_mm(6, 1, 0)
+        k_mm(5, 2)
+        k_mm(5, 1)
+        p_weave_dve(6, 0, 1)
+        y_weave(3, 0, True)
+        y_round(3, 1, False)
+        p_weave_mm(7, 0, 0)
+        p_scale(7, 1)
+        y_turn(3, 1)
+        p_weave_dve(6, 1, 1)
+        y_out(5, 2, True)
+        k_mm(5, 0)
+        p_weave_out(6, 1, 0)
+        y_store(4, 1)
+        y_out(5, 1, True)
+        y_quant(2)
+        p_weave_out(7, 0, 0)
+        y_weave(3, 1, True)
+        y_round(4, 0, False)
+        p_quant(6, 0)
+        y_out(5, 0, True)
+        k_mm(5, 3)
+        y_out(5, 3, True)
+        y_turn(4, 0)
+        y_store(5, 0)
+        p_quant(6, 1)
+        k_mm(6, 2)
+        p_weave_dve(7, 1, 0)
+        k_mm(6, 1)
+        p_weave_dve(7, 0, 1)
+        y_weave(4, 0, True)
+        y_round(4, 1, False)
+        y_turn(4, 1)
+        p_weave_dve(7, 1, 1)
+        y_out(6, 2, True)
+        k_mm(6, 0)
+        y_store(5, 1)
+        y_out(6, 1, True)
+        y_quant(3)
+        plane_store(0, 4)
+        y_weave(4, 1, True)
+        y_round(5, 0, False)
+        p_quant(7, 0)
+        y_out(6, 0, True)
+        k_mm(6, 3)
+        y_out(6, 3, True)
+        y_turn(5, 0)
+        y_store(6, 0)
+        p_quant(7, 1)
+        k_mm(7, 2)
+        k_mm(7, 1)
+        y_weave(5, 0, True)
+        y_round(5, 1, False)
+        y_turn(5, 1)
+        y_out(7, 2, False)
+        k_mm(7, 0)
+        y_store(6, 1)
+        y_out(7, 1, True)
+        y_quant(4)
+        y_weave(5, 1, True)
+        y_round(6, 0, False)
+        y_out(7, 0, False)
+        k_mm(7, 3)
+        y_out(7, 3, True)
+        y_turn(6, 0)
+        y_store(7, 0)
+        y_weave(6, 0, True)
+        y_round(6, 1, False)
+        y_turn(6, 1)
+        y_store(7, 1)
+        y_quant(5)
+        y_weave(6, 1, True)
+        y_round(7, 0, False)
+        y_turn(7, 0)
+        y_weave(7, 0, True)
+        y_round(7, 1, False)
+        y_turn(7, 1)
+        y_quant(6)
+        plane_store(4, 7)
+        y_weave(7, 1, True)
+        y_quant(7)
+        plane_store(7, 8)

@@ -61,32 +61,32 @@ def tile_linearrelationmeanjacobian_x2_kernel(
         live = {}
 
         def loads():
+            nc.sync.dma_start(out=gin_bf[:], in_=gin.rearrange("(p t) -> p t", t=PACK))
             nc.sync.dma_start(out=x_raw[0][:], in_=x[0:2].rearrange("r n d -> n r d"))
-            nc.scalar.dma_start(out=gin_bf[:], in_=gin.rearrange("(p t) -> p t", t=PACK))
-            for g in range(G):
-                cols = w1[:, g * K_PASS : (g + 1) * K_PASS]
-                nc.sync.dma_start(out=w1_raw[g][:], in_=cols.rearrange("(p j) h -> p j h", j=PACK))
             nc.scalar.dma_start(out=b1_bf[:], in_=b1.rearrange("(g p t) -> p g t", g=G, t=PACK))
             nc.scalar.dma_start(out=gamma_bf[:], in_=gamma.rearrange("(g p t) -> p g t", g=G, t=PACK))
             nc.scalar.dma_start(out=beta_bf[:], in_=beta.partition_broadcast(P))
+            for g in range(G):
+                cols = w1[:, g * K_PASS : (g + 1) * K_PASS]
+                nc.sync.dma_start(out=w1_raw[g][:], in_=cols.rearrange("(p j) h -> p j h", j=PACK))
             for q in range(1, PAIRS):
                 nc.sync.dma_start(out=x_raw[q][:], in_=x[2 * q : 2 * q + 2].rearrange("r n d -> n r d"))
             nc.sync.dma_start(
                 out=w2_codes[:].bitcast(I32),
                 in_=w2_words.rearrange("g p n t -> p g (n t)").bitcast(I32),
             )
+
+        def consts():
+            make_identity(nc, ident_f32[:])
+            nc.vector.memset(warm[:], 0.0)
+            nc.scalar.activation(out=warm_out[:], in_=warm[:], func=ACT.Silu)
+            make_identity(nc, ident_bf[:])
+            nc.gpsimd.memset(w2_plane[:].bitcast(I32), 0)
             for quad in range(4):
                 nc.sync.dma_start(
                     out=w2_plane[32 * quad : 32 * quad + 4].bitcast(I32),
                     in_=w2_scales[:, 4 * quad : 4 * quad + 4, :].rearrange("g q n -> q g n").bitcast(I32),
                 )
-
-        def consts():
-            make_identity(nc, ident_f32[:])
-            make_identity(nc, ident_bf[:])
-            nc.gpsimd.memset(w2_plane[:].bitcast(I32), 0)
-            nc.vector.memset(warm[:], 0.0)
-            nc.scalar.activation(out=warm_out[:], in_=warm[:], func=ACT.Silu)
 
         def small_act():
             nc.scalar.activation(out=b1_half[:], in_=b1_bf[:], func=ACT.Copy, scale=0.5)
@@ -231,9 +231,9 @@ def tile_linearrelationmeanjacobian_x2_kernel(
             live["rows", r, g] = rows
 
         def grouped(r, g):
-            if ("grouped", r, g) not in live:
-                live["grouped", r, g] = work.tile([P, D, PACK], BF16, name="p_grouped", bufs=4, align_bytes=64)
-            return live["grouped", r, g]
+            if ("grouped", r) not in live:
+                live["grouped", r] = work.tile([P, G, D, PACK], BF16, name="p_grouped", bufs=3, align_bytes=64)
+            return live["grouped", r][:, g]
 
         def p_weave_dve(r, g, half):
             cols = slice(half * 256, (half + 1) * 256)
@@ -267,25 +267,27 @@ def tile_linearrelationmeanjacobian_x2_kernel(
                 in_=live["weave", r, g, half][:].rearrange("p s d t -> p (s d t)"),
             )
 
-        def p_quant(r, g):
-            codes = work.tile([P, D], U32, name="p_codes", bufs=6, align_bytes=64)
-            scales = work.tile([P, D], U8, name="p_scales", bufs=6, align_bytes=64)
+        def p_quant(r, g0, g1):
+            if ("p", r) not in live:
+                codes = work.tile([P, G, D], U32, name="p_codes", bufs=3, align_bytes=64)
+                scales = work.tile([P, G, D], U8, name="p_scales", bufs=3, align_bytes=64)
+                live["p", r] = (codes, scales)
+            codes, scales = live["p", r]
             nc.vector.quantize_mx(
-                out=codes[:].bitcast(FP8X4),
-                scales=scales[:],
-                in_=live["grouped", r, g][:].rearrange("p d t -> p (d t)"),
+                out=codes[:, g0:g1].rearrange("p g d -> p (g d)").bitcast(FP8X4),
+                scales=scales[:, g0:g1].rearrange("p g d -> p (g d)"),
+                in_=live["grouped", r][:, g0:g1].rearrange("p g d t -> p (g d t)"),
             )
-            live["p", r, g] = (codes, scales)
 
         def k_mm(r, j):
-            bank = psum.tile([P, O], F32, name="k_bank", tag="k")
+            bank = psum.tile([P, O], F32, name="k_bank", tag="pre" if r == R - 1 and j >= 2 else "k")
             cols = slice(j * P, (j + 1) * P)
             for g in range(G):
-                codes, scales = live["p", r, g]
+                codes, scales = live["p", r]
                 nc.tensor.matmul_mx(
                     out=bank[:],
-                    lhsT=codes[:, cols].bitcast(FP8X4),
-                    lhsT_scale=scales[:, cols],
+                    lhsT=codes[:, g, cols].bitcast(FP8X4),
+                    lhsT_scale=scales[:, g, cols],
                     rhs=w2_codes[:, g, :].bitcast(FP8X4),
                     rhs_scale=w2_plane[:, g, :],
                     start=(g == 0),
@@ -294,33 +296,33 @@ def tile_linearrelationmeanjacobian_x2_kernel(
             live["k", r, j] = bank
 
         def y_out(r, j, on_scalar):
-            if ("y", r, j // 2) not in live:
-                live["y", r, j // 2] = work.tile([P, 2, O], F32, name="y", bufs=5)
-            y = live["y", r, j // 2]
+            if ("y", r) not in live:
+                live["y", r] = work.tile([P, PACK, O], F32, name="y", bufs=3)
+            y = live["y", r]
             gain = out_gain[:, r, j : j + 1]
             if on_scalar:
-                nc.scalar.activation(out=y[:, j % 2, :], in_=live["k", r, j][:], func=ACT.Copy, scale=gain)
+                nc.scalar.activation(out=y[:, j, :], in_=live["k", r, j][:], func=ACT.Copy, scale=gain)
             else:
                 nc.vector.tensor_scalar(
-                    out=y[:, j % 2, :], in0=live["k", r, j][:], scalar1=gain, scalar2=None, op0=ALU.mult
+                    out=y[:, j, :], in0=live["k", r, j][:], scalar1=gain, scalar2=None, op0=ALU.mult
                 )
 
-        def y_store(r, half):
+        def y_store(r, j0, j1):
             rows = out_0[r].rearrange("(c j) o -> c j o", j=PACK)
-            nc.sync.dma_start(out=rows[:, 2 * half : 2 * half + 2, :], in_=live["y", r, half][:])
+            nc.sync.dma_start(out=rows[:, j0:j1, :], in_=live["y", r][:, j0:j1, :])
 
-        def y_round(r, half, on_scalar):
-            if ("y_bf", r, half) not in live:
-                live["y_bf", r, half] = work.tile([P, 2, O], BF16, name="y_bf", bufs=3)
-            y_bf = live["y_bf", r, half]
+        def y_round(r, j0, j1, on_scalar):
+            if ("y_bf", r) not in live:
+                live["y_bf", r] = work.tile([P, PACK, O], BF16, name="y_bf", bufs=2)
+            y_bf = live["y_bf", r]
             if on_scalar:
-                nc.scalar.copy(out=y_bf[:], in_=live["y", r, half][:])
+                nc.scalar.copy(out=y_bf[:, j0:j1, :], in_=live["y", r][:, j0:j1, :])
             else:
-                nc.vector.tensor_copy(out=y_bf[:], in_=live["y", r, half][:])
+                nc.vector.tensor_copy(out=y_bf[:, j0:j1, :], in_=live["y", r][:, j0:j1, :])
 
         def y_turn(r, half):
             bank = psum.tile([P, 2, 2, P], F32, name="y_bank", tag="turn")
-            words = live["y_bf", r, half][:].bitcast(F32)
+            words = live["y_bf", r][:, 2 * half : 2 * half + 2, :].bitcast(F32)
             for jl in range(2):
                 for u in range(2):
                     nc.tensor.transpose(bank[:, jl, u, :], words[:, jl, u : O // 2 : 2], ident_f32[:])
@@ -351,347 +353,326 @@ def tile_linearrelationmeanjacobian_x2_kernel(
         def plane_store(r0, r1):
             cols = slice(r0 * D, r1 * D)
             for quad in range(4):
-                nc.sync.dma_start(
+                queue = nc.scalar if r1 == R else nc.sync
+                queue.dma_start(
                     out=out_2[0, 4 * quad : 4 * quad + 4, cols].bitcast(I32),
                     in_=out_plane[32 * quad : 32 * quad + 4, cols].bitcast(I32),
                 )
 
 
-        consts()
         loads()
+        small_act()
+        consts()
+        w1_group(0, 0, 2, True)
         x_turn(0)
         x_gain(0)
-        x_quant(0)
-        w1_group(0, 0, 2, False)
-        w1_group(1, 2, 4, False)
-        w1_group(0, 2, 4, True)
+        w1_group(0, 2, 4, False)
         w1_turn(0, 0)
-        w1_turn(0, 1)
-        w1_quant(0, 0, 2)
-        x_turn(1)
-        w1_quant(1, 2, 4)
-        x_gain(1)
-        small_dve()
-        w1_quant(0, 2, 4)
-        x_quant(1)
         w1_out(0, 0, True)
+        x_quant(0)
+        small_dve()
+        w1_quant(0, 0, 2)
+        w1_quant(0, 2, 4)
+        w1_turn(1, 1)
+        w1_group(1, 2, 4, True)
+        x_turn(1)
         w1_group(1, 0, 2, False)
-        small_act()
+        x_gain(1)
+        x_quant(1)
+        pre_mm(0, 0, 0)
+        w1_out(1, 1, True)
         x_turn(2)
         x_gain(2)
-        w1_quant(1, 0, 2)
-        x_quant(2)
-        pre_mm(0, 0, 0)
-        pre_mm(0, 0, 1)
-        x_turn(3)
-        w1_out(0, 1, True)
+        w1_quant(1, 0, 4)
         pre_act(0, 0, 0)
-        w1_turn(1, 0)
-        pre_act(0, 0, 2)
-        x_gain(3)
         pre_act(0, 0, 1)
-        pre_mm(0, 1, 0)
+        pre_mm(0, 0, 1)
         pre_prod(0, 0, 0)
+        pre_mm(0, 1, 0)
+        x_quant(2)
         pre_act(0, 0, 3)
-        pre_mm(0, 1, 1)
-        pre_prod(0, 0, 2)
-        pre_act(0, 1, 0)
-        w1_turn(1, 1)
-        w1_out(1, 0, False)
+        w1_turn(0, 1)
+        pre_act(0, 0, 2)
         pre_prod(0, 0, 1)
         pre_prod(0, 0, 3)
-        pre_act(0, 1, 2)
+        pre_prod(0, 0, 2)
+        pre_act(0, 1, 0)
         pre_act(0, 1, 1)
-        x_quant(3)
-        pre_mm(1, 0, 0)
+        pre_mm(0, 1, 1)
         pre_prod(0, 1, 0)
+        w1_turn(1, 0)
+        pre_mm(1, 0, 0)
         pre_act(0, 1, 3)
-        pre_mm(1, 0, 1)
+        pre_act(0, 1, 2)
+        pre_prod(0, 1, 1)
+        w1_out(0, 1, True)
         slope(0, 0)
+        pre_prod(0, 1, 3)
+        x_turn(3)
+        x_gain(3)
+        p_scale(0, 0)
         pre_prod(0, 1, 2)
         pre_act(1, 0, 0)
-        p_scale(0, 0)
-        pre_prod(0, 1, 1)
-        pre_prod(0, 1, 3)
-        pre_act(1, 0, 2)
-        p_weave_dve(0, 0, 0)
-        w1_out(1, 1, True)
         pre_act(1, 0, 1)
-        pre_mm(1, 1, 0)
+        pre_mm(1, 0, 1)
         pre_prod(1, 0, 0)
+        pre_mm(1, 1, 0)
+        x_quant(3)
+        p_weave_mm(0, 0, 1)
         pre_act(1, 0, 3)
-        pre_mm(1, 1, 1)
-        slope(0, 1)
-        pre_prod(1, 0, 2)
-        p_scale(0, 1)
-        pre_act(1, 1, 0)
-        p_scale(1, 0)
-        p_weave_mm(0, 1, 1)
+        pre_act(1, 0, 2)
         pre_prod(1, 0, 1)
+        slope(0, 1)
         pre_prod(1, 0, 3)
-        pre_act(1, 1, 2)
-        p_weave_dve(1, 0, 0)
+        w1_out(1, 0, True)
+        p_scale(1, 0)
+        pre_prod(1, 0, 2)
+        p_weave_mm(0, 0, 0)
+        pre_act(1, 1, 0)
         pre_act(1, 1, 1)
-        p_weave_mm(0, 1, 0)
-        pre_mm(2, 0, 0)
-        p_weave_out(0, 1, 1)
+        p_weave_out(0, 0, 1)
+        p_scale(0, 1)
+        pre_mm(1, 1, 1)
         pre_prod(1, 1, 0)
+        pre_mm(2, 0, 0)
+        p_weave_mm(1, 0, 1)
         pre_act(1, 1, 3)
-        pre_mm(2, 0, 1)
-        slope(1, 0)
-        p_weave_dve(0, 0, 1)
-        pre_prod(1, 1, 2)
-        p_scale(1, 1)
-        pre_act(2, 0, 0)
-        p_scale(2, 0)
-        p_weave_out(0, 1, 0)
-        p_weave_mm(1, 1, 1)
+        pre_act(1, 1, 2)
         pre_prod(1, 1, 1)
+        p_weave_dve_all(0, 1)
+        slope(1, 0)
         pre_prod(1, 1, 3)
-        pre_act(2, 0, 2)
-        p_quant(0, 0)
-        p_quant(0, 1)
+        p_weave_out(0, 0, 0)
+        p_scale(2, 0)
+        pre_prod(1, 1, 2)
+        p_weave_mm(1, 0, 0)
+        p_quant(0, 0, 2)
+        pre_act(2, 0, 0)
         pre_act(2, 0, 1)
-        p_weave_mm(1, 1, 0)
-        pre_mm(2, 1, 0)
-        p_weave_out(1, 1, 1)
-        k_mm(0, 2)
+        p_weave_out(1, 0, 1)
+        p_scale(1, 1)
+        pre_mm(2, 0, 1)
         pre_prod(2, 0, 0)
+        pre_mm(2, 1, 0)
+        p_weave_mm(2, 0, 1)
         pre_act(2, 0, 3)
-        pre_mm(2, 1, 1)
-        k_mm(0, 1)
-        slope(1, 1)
-        p_weave_dve(1, 0, 1)
-        p_weave_mm(2, 0, 0)
-        pre_prod(2, 0, 2)
-        p_scale(2, 1)
-        y_out(0, 2, True)
-        pre_act(2, 1, 0)
-        p_scale(3, 0)
-        k_mm(0, 0)
-        p_weave_out(1, 1, 0)
-        p_weave_mm(2, 1, 1)
-        y_out(0, 1, True)
+        pre_act(2, 0, 2)
         pre_prod(2, 0, 1)
-        p_weave_out(2, 0, 0)
+        p_weave_dve_all(1, 1)
+        slope(1, 1)
+        k_mm(0, 0)
         pre_prod(2, 0, 3)
-        pre_act(2, 1, 2)
-        p_quant(1, 0)
+        p_weave_out(1, 0, 0)
+        p_scale(3, 0)
+        pre_prod(2, 0, 2)
         y_out(0, 0, True)
-        k_mm(0, 3)
-        y_out(0, 3, True)
-        y_store(0, 0)
-        p_quant(1, 1)
+        k_mm(0, 1)
+        p_weave_mm(2, 0, 0)
+        y_out(0, 1, True)
+        p_quant(1, 0, 2)
+        pre_act(2, 1, 0)
         pre_act(2, 1, 1)
-        pre_mm(3, 0, 0)
-        p_weave_out(2, 1, 1)
-        k_mm(1, 2)
+        p_weave_out(2, 0, 1)
+        p_scale(2, 1)
+        pre_mm(2, 1, 1)
+        k_mm(0, 2)
         pre_prod(2, 1, 0)
+        y_out(0, 2, True)
+        k_mm(0, 3)
+        pre_mm(3, 0, 0)
+        y_out(0, 3, True)
+        p_weave_mm(3, 0, 1)
         pre_act(2, 1, 3)
-        pre_mm(3, 0, 1)
-        p_weave_dve(2, 1, 0)
-        k_mm(1, 1)
-        slope(2, 0)
-        p_weave_dve(2, 0, 1)
-        p_weave_mm(3, 0, 0)
-        pre_prod(2, 1, 2)
-        p_scale(3, 1)
-        y_out(1, 2, True)
-        pre_act(3, 0, 0)
-        p_scale(4, 0)
-        k_mm(1, 0)
-        y_store(0, 1)
-        y_out(1, 1, True)
+        pre_act(2, 1, 2)
         pre_prod(2, 1, 1)
-        p_weave_out(3, 0, 0)
+        p_weave_dve_all(2, 1)
+        slope(2, 0)
+        k_mm(1, 0)
         pre_prod(2, 1, 3)
-        y_round(0, 0, False)
-        pre_act(3, 0, 2)
-        p_quant(2, 0)
+        y_store(0, 0, 2)
+        p_weave_out(2, 0, 0)
+        p_scale(4, 0)
+        pre_prod(2, 1, 2)
         y_out(1, 0, True)
-        k_mm(1, 3)
-        y_out(1, 3, True)
-        y_turn(0, 0)
-        y_store(1, 0)
-        p_quant(2, 1)
+        k_mm(1, 1)
+        p_weave_mm(3, 0, 0)
+        y_out(1, 1, True)
+        p_quant(2, 0, 2)
+        pre_act(3, 0, 0)
         pre_act(3, 0, 1)
-        pre_mm(3, 1, 0)
-        k_mm(2, 2)
+        p_weave_out(3, 0, 1)
+        p_scale(3, 1)
+        pre_mm(3, 0, 1)
+        k_mm(1, 2)
         pre_prod(3, 0, 0)
+        y_out(1, 2, True)
+        k_mm(1, 3)
+        pre_mm(3, 1, 0)
+        y_out(1, 3, True)
+        p_weave_mm(4, 0, 1)
         pre_act(3, 0, 3)
-        pre_mm(3, 1, 1)
-        p_weave_dve(3, 1, 0)
-        k_mm(2, 1)
-        slope(2, 1)
-        p_weave_dve(3, 0, 1)
-        y_weave(0, 0, True)
-        y_round(0, 1, False)
-        p_weave_mm(4, 0, 0)
-        pre_prod(3, 0, 2)
-        p_scale(4, 1)
-        y_turn(0, 1)
-        p_weave_dve(3, 1, 1)
-        y_out(2, 2, True)
-        pre_act(3, 1, 0)
-        p_scale(5, 0)
-        k_mm(2, 0)
-        p_weave_mm(4, 1, 1)
-        y_store(1, 1)
-        y_out(2, 1, True)
+        pre_act(3, 0, 2)
         pre_prod(3, 0, 1)
-        p_weave_out(4, 0, 0)
+        p_weave_dve_all(3, 1)
+        slope(2, 1)
+        k_mm(2, 0)
         pre_prod(3, 0, 3)
-        y_weave(0, 1, True)
-        y_round(1, 0, False)
-        pre_act(3, 1, 2)
-        p_quant(3, 0)
+        y_store(1, 0, 2)
+        p_weave_out(3, 0, 0)
+        p_scale(5, 0)
+        pre_prod(3, 0, 2)
+        y_store(0, 2, 4)
         y_out(2, 0, True)
-        k_mm(2, 3)
-        y_out(2, 3, True)
-        y_turn(1, 0)
-        y_store(2, 0)
-        p_quant(3, 1)
+        k_mm(2, 1)
+        p_weave_mm(4, 0, 0)
+        y_out(2, 1, True)
+        p_quant(3, 0, 2)
+        pre_act(3, 1, 0)
         pre_act(3, 1, 1)
-        p_weave_mm(4, 1, 0)
-        p_weave_out(4, 1, 1)
-        k_mm(3, 2)
+        p_weave_out(4, 0, 1)
+        p_scale(4, 1)
+        pre_mm(3, 1, 1)
+        k_mm(2, 2)
         pre_prod(3, 1, 0)
+        y_out(2, 2, True)
+        k_mm(2, 3)
+        y_round(0, 2, 4, False)
+        y_out(2, 3, True)
+        p_weave_mm(5, 0, 1)
         pre_act(3, 1, 3)
-        k_mm(3, 1)
-        slope(3, 0)
-        p_weave_dve(4, 0, 1)
-        y_weave(1, 0, True)
-        y_round(1, 1, False)
-        p_weave_mm(5, 0, 0)
-        pre_prod(3, 1, 2)
-        p_scale(5, 1)
-        y_turn(1, 1)
-        y_out(3, 2, True)
-        p_scale(6, 0)
-        k_mm(3, 0)
-        p_weave_out(4, 1, 0)
-        y_store(2, 1)
-        y_out(3, 1, True)
+        pre_act(3, 1, 2)
         pre_prod(3, 1, 1)
-        y_quant(0)
-        p_weave_out(5, 0, 0)
+        p_weave_dve_all(4, 1)
+        slope(3, 0)
+        k_mm(3, 0)
         pre_prod(3, 1, 3)
-        y_weave(1, 1, True)
-        y_round(2, 0, False)
-        p_quant(4, 0)
+        y_store(2, 0, 2)
+        p_weave_out(4, 0, 0)
+        p_scale(6, 0)
+        pre_prod(3, 1, 2)
+        y_store(1, 2, 4)
+        y_round(0, 0, 2, True)
         y_out(3, 0, True)
+        k_mm(3, 1)
+        p_weave_mm(5, 0, 0)
+        y_out(3, 1, True)
+        p_quant(4, 0, 2)
+        y_turn(0, 1)
+        p_weave_out(5, 0, 1)
+        p_scale(5, 1)
+        k_mm(3, 2)
+        y_out(3, 2, True)
         k_mm(3, 3)
+        y_round(1, 2, 4, False)
         y_out(3, 3, True)
-        y_turn(2, 0)
-        y_store(3, 0)
-        p_quant(4, 1)
-        p_weave_mm(5, 1, 0)
-        k_mm(4, 2)
-        k_mm(4, 1)
+        p_weave_mm(6, 0, 1)
+        y_turn(0, 0)
+        p_weave_dve_all(5, 1)
         slope(3, 1)
-        p_weave_dve(5, 0, 1)
-        y_weave(2, 0, True)
-        y_round(2, 1, False)
-        p_weave_mm(6, 0, 0)
-        p_scale(6, 1)
-        y_turn(2, 1)
-        p_weave_dve(5, 1, 1)
-        y_out(4, 2, True)
-        p_scale(7, 0)
         k_mm(4, 0)
-        p_weave_out(5, 1, 0)
-        y_store(3, 1)
-        y_out(4, 1, True)
-        y_quant(1)
-        p_weave_out(6, 0, 0)
-        y_weave(2, 1, True)
-        y_round(3, 0, False)
-        p_quant(5, 0)
+        y_weave(0, 1, True)
+        y_store(3, 0, 2)
+        p_weave_out(5, 0, 0)
+        p_scale(7, 0)
+        y_store(2, 2, 4)
+        y_round(1, 0, 2, True)
         y_out(4, 0, True)
+        k_mm(4, 1)
+        p_weave_mm(6, 0, 0)
+        y_out(4, 1, True)
+        p_quant(5, 0, 2)
+        y_turn(1, 1)
+        y_weave(0, 0, True)
+        p_weave_out(6, 0, 1)
+        p_scale(6, 1)
+        k_mm(4, 2)
+        y_out(4, 2, True)
         k_mm(4, 3)
+        y_round(2, 2, 4, False)
         y_out(4, 3, True)
-        y_turn(3, 0)
-        y_store(4, 0)
-        p_quant(5, 1)
-        p_weave_mm(6, 1, 0)
-        k_mm(5, 2)
-        k_mm(5, 1)
-        p_weave_dve(6, 0, 1)
-        y_weave(3, 0, True)
-        y_round(3, 1, False)
-        p_weave_mm(7, 0, 0)
-        p_scale(7, 1)
-        y_turn(3, 1)
-        p_weave_dve(6, 1, 1)
-        y_out(5, 2, True)
+        p_weave_mm(7, 0, 1)
+        y_turn(1, 0)
+        p_weave_dve_all(6, 1)
         k_mm(5, 0)
-        p_weave_out(6, 1, 0)
-        y_store(4, 1)
-        y_out(5, 1, True)
-        y_quant(2)
-        p_weave_out(7, 0, 0)
-        y_weave(3, 1, True)
-        y_round(4, 0, False)
-        p_quant(6, 0)
+        y_weave(1, 1, True)
+        y_store(4, 0, 2)
+        p_weave_out(6, 0, 0)
+        y_store(3, 2, 4)
+        y_round(2, 0, 2, True)
         y_out(5, 0, True)
+        k_mm(5, 1)
+        y_quant(0)
+        p_weave_mm(7, 0, 0)
+        y_out(5, 1, True)
+        p_quant(6, 0, 2)
+        y_turn(2, 1)
+        y_weave(1, 0, True)
+        p_weave_out(7, 0, 1)
+        p_scale(7, 1)
+        k_mm(5, 2)
+        y_out(5, 2, True)
         k_mm(5, 3)
+        y_round(3, 0, 4, False)
         y_out(5, 3, True)
-        y_turn(4, 0)
-        y_store(5, 0)
-        p_quant(6, 1)
-        k_mm(6, 2)
-        p_weave_dve(7, 1, 0)
-        k_mm(6, 1)
-        p_weave_dve(7, 0, 1)
-        y_weave(4, 0, True)
-        y_round(4, 1, False)
-        y_turn(4, 1)
-        p_weave_dve(7, 1, 1)
-        y_out(6, 2, True)
+        y_turn(2, 0)
+        p_weave_dve_all(7, 1)
         k_mm(6, 0)
-        y_store(5, 1)
+        y_weave(2, 1, True)
+        y_store(5, 0, 2)
+        p_weave_out(7, 0, 0)
+        y_store(4, 2, 4)
+        y_out(6, 0, False)
+        k_mm(6, 1)
+        y_quant(1)
         y_out(6, 1, True)
-        y_quant(3)
-        plane_store(0, 4)
-        y_weave(4, 1, True)
-        y_round(5, 0, False)
-        p_quant(7, 0)
-        y_out(6, 0, True)
+        y_turn(3, 1)
+        y_weave(2, 0, True)
+        p_quant(7, 0, 2)
+        k_mm(6, 2)
+        y_out(6, 2, True)
         k_mm(6, 3)
+        y_round(4, 0, 4, False)
         y_out(6, 3, True)
-        y_turn(5, 0)
-        y_store(6, 0)
-        p_quant(7, 1)
-        k_mm(7, 2)
+        y_turn(3, 0)
         k_mm(7, 1)
-        y_weave(5, 0, True)
-        y_round(5, 1, False)
-        y_turn(5, 1)
-        y_out(7, 2, False)
-        k_mm(7, 0)
-        y_store(6, 1)
-        y_out(7, 1, True)
-        y_quant(4)
-        y_weave(5, 1, True)
-        y_round(6, 0, False)
-        y_out(7, 0, False)
+        y_weave(3, 1, True)
+        y_store(6, 0, 2)
+        y_store(5, 2, 4)
+        y_quant(2)
         k_mm(7, 3)
+        k_mm(7, 0)
+        y_turn(4, 1)
+        y_weave(3, 0, True)
+        y_out(7, 1, True)
+        y_round(5, 0, 4, False)
         y_out(7, 3, True)
-        y_turn(6, 0)
-        y_store(7, 0)
-        y_weave(6, 0, True)
-        y_round(6, 1, False)
+        y_turn(4, 0)
+        y_weave(4, 1, True)
+        y_store(6, 2, 4)
+        y_quant(3)
+        k_mm(7, 2)
+        y_out(7, 0, False)
+        y_turn(5, 1)
+        y_weave(4, 0, True)
+        y_round(6, 0, 4, False)
+        y_store(7, 0, 2)
+        y_turn(5, 0)
+        y_out(7, 2, True)
+        y_weave(5, 1, True)
+        y_quant(4)
+        y_store(7, 2, 4)
         y_turn(6, 1)
-        y_store(7, 1)
-        y_quant(5)
+        y_weave(5, 0, True)
+        y_round(7, 0, 4, False)
+        y_turn(6, 0)
         y_weave(6, 1, True)
-        y_round(7, 0, False)
-        y_turn(7, 0)
-        y_weave(7, 0, True)
-        y_round(7, 1, False)
-        y_turn(7, 1)
+        y_quant(5)
+        plane_store(0, 6)
+        y_weave(6, 0, True)
         y_quant(6)
-        plane_store(4, 7)
+        y_turn(7, 0)
+        y_weave(7, 0, False)
+        y_turn(7, 1)
         y_weave(7, 1, True)
         y_quant(7)
-        plane_store(7, 8)
+        plane_store(6, 8)

@@ -20,6 +20,7 @@ PACK = 4
 K_PASS = P * PACK
 G = H // K_PASS
 PAIRS = R // 2
+LATE = 8
 
 
 def tile_linearrelationmeanjacobian_x2_kernel(
@@ -61,14 +62,15 @@ def tile_linearrelationmeanjacobian_x2_kernel(
         live = {}
 
         def loads():
-            nc.sync.dma_start(out=gin_bf[:], in_=gin.rearrange("(p t) -> p t", t=PACK))
-            nc.sync.dma_start(out=x_raw[0][:], in_=x[0:2].rearrange("r n d -> n r d"))
+            nc.scalar.dma_start(out=gin_bf[:], in_=gin.rearrange("(p t) -> p t", t=PACK))
             nc.scalar.dma_start(out=b1_bf[:], in_=b1.rearrange("(g p t) -> p g t", g=G, t=PACK))
             nc.scalar.dma_start(out=gamma_bf[:], in_=gamma.rearrange("(g p t) -> p g t", g=G, t=PACK))
             nc.scalar.dma_start(out=beta_bf[:], in_=beta.partition_broadcast(P))
             for g in range(G):
                 cols = w1[:, g * K_PASS : (g + 1) * K_PASS]
                 nc.sync.dma_start(out=w1_raw[g][:], in_=cols.rearrange("(p j) h -> p j h", j=PACK))
+                if g == 0:
+                    nc.sync.dma_start(out=x_raw[0][:], in_=x[0:2].rearrange("r n d -> n r d"))
             for q in range(1, PAIRS):
                 nc.sync.dma_start(out=x_raw[q][:], in_=x[2 * q : 2 * q + 2].rearrange("r n d -> n r d"))
             nc.sync.dma_start(
@@ -172,53 +174,55 @@ def tile_linearrelationmeanjacobian_x2_kernel(
                 )
             live["pre", q, g, half] = bank
 
-        def pre_act(q, g, t):
-            bank = live["pre", q, g, t // 2]
-            silu = work.tile([P, 2, N], F32, name="silu", bufs=4)
-            tanh = work.tile([P, 2, N], F32, name="tanh", bufs=4)
-            for i in range(2):
+        def pre_act(q, g, half):
+            bank = live["pre", q, g, half]
+            silu = work.tile([P, 2, 2, N], F32, name="silu", bufs=4)
+            tanh = work.tile([P, 2, 2, N], F32, name="tanh", bufs=4)
+            for tl in range(2):
+                t = 2 * half + tl
                 nc.scalar.activation(
-                    out=tanh[:, i, :],
-                    in_=bank[:, t % 2, i * N : (i + 1) * N],
-                    func=ACT.Tanh,
-                    bias=b1_half[:, g, t : t + 1],
-                    scale=0.5,
-                    accum_out=tanh_sum[:, q, g, t, i : i + 1],
+                    out=silu[:, tl].rearrange("p i n -> p (i n)"),
+                    in_=bank[:, tl, :],
+                    func=ACT.Silu,
+                    bias=b1_full[:, g, t : t + 1],
                 )
-            nc.scalar.activation(
-                out=silu[:].rearrange("p i n -> p (i n)"),
-                in_=bank[:, t % 2, :],
-                func=ACT.Silu,
-                bias=b1_full[:, g, t : t + 1],
-            )
-            live["st", q, g, t] = (silu, tanh)
+                for i in range(2):
+                    nc.scalar.activation(
+                        out=tanh[:, tl, i, :],
+                        in_=bank[:, tl, i * N : (i + 1) * N],
+                        func=ACT.Tanh,
+                        bias=b1_half[:, g, t : t + 1],
+                        scale=0.5,
+                        accum_out=tanh_sum[:, q, g, t, i : i + 1],
+                    )
+            live["st", q, g, half] = (silu, tanh)
 
-        def pre_prod(q, g, t):
-            silu, tanh = live["st", q, g, t]
-            prod = work.tile([P, 2, N], F32, name="prod")
-            for i in range(2):
-                nc.vector.scalar_tensor_tensor(
-                    out=prod[:, i, :],
-                    in0=tanh[:, i, :],
-                    scalar=1.0,
-                    in1=silu[:, i, :],
-                    op0=ALU.subtract,
-                    op1=ALU.mult,
-                    accum_out=prod_sum[:, q, g, t, i : i + 1],
-                )
+        def pre_prod(q, g, half):
+            silu, tanh = live["st", q, g, half]
+            for tl in (1, 0):
+                for i in (1, 0):
+                    nc.vector.scalar_tensor_tensor(
+                        out=silu[:, tl, i, :],
+                        in0=tanh[:, tl, i, :],
+                        scalar=1.0,
+                        in1=silu[:, tl, i, :],
+                        op0=ALU.subtract,
+                        op1=ALU.mult,
+                        accum_out=prod_sum[:, q, g, 2 * half + tl, i : i + 1],
+                    )
 
-        def slope(q, g):
+        def slope(q, g0, g1):
             nc.vector.scalar_tensor_tensor(
-                out=slope_sum[:, q, g].rearrange("p t i -> p (t i)"),
-                in0=tanh_sum[:, q, g].rearrange("p t i -> p (t i)"),
+                out=slope_sum[:, q, g0:g1].rearrange("p g t i -> p (g t i)"),
+                in0=tanh_sum[:, q, g0:g1].rearrange("p g t i -> p (g t i)"),
                 scalar=float(N),
-                in1=prod_sum[:, q, g].rearrange("p t i -> p (t i)"),
+                in1=prod_sum[:, q, g0:g1].rearrange("p g t i -> p (g t i)"),
                 op0=ALU.add,
                 op1=ALU.subtract,
             )
 
         def p_scale(r, g):
-            rows = work.tile([P, PACK, D], BF16, name="p_rows", bufs=4)
+            rows = work.tile([P, PACK, D], BF16, name="p_rows", bufs=3)
             for t in range(PACK):
                 nc.vector.tensor_scalar(
                     out=rows[:, t, :],
@@ -280,7 +284,7 @@ def tile_linearrelationmeanjacobian_x2_kernel(
             )
 
         def k_mm(r, j):
-            bank = psum.tile([P, O], F32, name="k_bank", tag="pre" if r == R - 1 and j >= 2 else "k")
+            bank = psum.tile([P, O], F32, name="k_bank", tag="weave" if r == R - 1 and j >= 2 else "k")
             cols = slice(j * P, (j + 1) * P)
             for g in range(G):
                 codes, scales = live["p", r]
@@ -297,7 +301,7 @@ def tile_linearrelationmeanjacobian_x2_kernel(
 
         def y_out(r, j, on_scalar):
             if ("y", r) not in live:
-                live["y", r] = work.tile([P, PACK, O], F32, name="y", bufs=3)
+                live["y", r] = work.tile([P, PACK, O], F32, name="y", bufs=R)
             y = live["y", r]
             gain = out_gain[:, r, j : j + 1]
             if on_scalar:
@@ -313,7 +317,7 @@ def tile_linearrelationmeanjacobian_x2_kernel(
 
         def y_round(r, j0, j1, on_scalar):
             if ("y_bf", r) not in live:
-                live["y_bf", r] = work.tile([P, PACK, O], BF16, name="y_bf", bufs=2)
+                live["y_bf", r] = work.tile([P, PACK, O], BF16, name="y_bf", bufs=3)
             y_bf = live["y_bf", r]
             if on_scalar:
                 nc.scalar.copy(out=y_bf[:, j0:j1, :], in_=live["y", r][:, j0:j1, :])
@@ -321,7 +325,7 @@ def tile_linearrelationmeanjacobian_x2_kernel(
                 nc.vector.tensor_copy(out=y_bf[:, j0:j1, :], in_=live["y", r][:, j0:j1, :])
 
         def y_turn(r, half):
-            bank = psum.tile([P, 2, 2, P], F32, name="y_bank", tag="turn")
+            bank = psum.tile([P, 2, 2, P], F32, name="y_bank", tag="pre" if r >= LATE and half == 1 else "turn")
             words = live["y_bf", r][:, 2 * half : 2 * half + 2, :].bitcast(F32)
             for jl in range(2):
                 for u in range(2):
@@ -330,7 +334,7 @@ def tile_linearrelationmeanjacobian_x2_kernel(
 
         def y_weave(r, half, on_scalar):
             if ("y_grouped", r) not in live:
-                live["y_grouped", r] = work.tile([P, P, PACK, 2], F32, name="y_grouped", align_bytes=64)
+                live["y_grouped", r] = work.tile([P, P, PACK, 2], F32, name="y_grouped", bufs=3, align_bytes=64)
             dst = live["y_grouped", r][:, :, 2 * half : 2 * half + 2, :]
             src = live["y_bank", r, half][:].rearrange("p j u c -> p c j u")
             if on_scalar:
@@ -339,7 +343,7 @@ def tile_linearrelationmeanjacobian_x2_kernel(
                 nc.vector.tensor_copy(out=dst, in_=src)
 
         def y_quant(r):
-            codes = work.tile([P, D], U32, name="y_codes", bufs=3, align_bytes=64)
+            codes = work.tile([P, D], U32, name="y_codes", bufs=R, align_bytes=64)
             cols = slice(r * D, (r + 1) * D)
             nc.vector.quantize_mx(
                 out=codes[:].bitcast(FP8X4),
@@ -363,316 +367,283 @@ def tile_linearrelationmeanjacobian_x2_kernel(
         loads()
         small_act()
         consts()
-        w1_group(0, 0, 2, True)
-        x_turn(0)
-        x_gain(0)
-        w1_group(0, 2, 4, False)
         w1_turn(0, 0)
+        w1_group(0, 0, 2, False)
         w1_out(0, 0, True)
-        x_quant(0)
-        small_dve()
+        w1_group(1, 0, 2, True)
+        x_turn(0)
+        w1_turn(0, 1)
+        w1_group(0, 2, 4, False)
         w1_quant(0, 0, 2)
         w1_quant(0, 2, 4)
-        w1_turn(1, 1)
-        w1_group(1, 2, 4, True)
+        x_gain(0)
         x_turn(1)
-        w1_group(1, 0, 2, False)
+        small_dve()
+        x_quant(0)
+        w1_group(1, 2, 4, False)
         x_gain(1)
-        x_quant(1)
-        pre_mm(0, 0, 0)
-        w1_out(1, 1, True)
-        x_turn(2)
-        x_gain(2)
         w1_quant(1, 0, 4)
-        pre_act(0, 0, 0)
-        pre_act(0, 0, 1)
-        pre_mm(0, 0, 1)
-        pre_prod(0, 0, 0)
-        pre_mm(0, 1, 0)
-        x_quant(2)
-        pre_act(0, 0, 3)
-        w1_turn(0, 1)
-        pre_act(0, 0, 2)
-        pre_prod(0, 0, 1)
-        pre_prod(0, 0, 3)
-        pre_prod(0, 0, 2)
-        pre_act(0, 1, 0)
-        pre_act(0, 1, 1)
-        pre_mm(0, 1, 1)
-        pre_prod(0, 1, 0)
-        w1_turn(1, 0)
-        pre_mm(1, 0, 0)
-        pre_act(0, 1, 3)
-        pre_act(0, 1, 2)
-        pre_prod(0, 1, 1)
         w1_out(0, 1, True)
-        slope(0, 0)
-        pre_prod(0, 1, 3)
+        pre_mm(0, 0, 0)
+        x_turn(2)
+        pre_act(0, 0, 0)
+        pre_mm(0, 0, 1)
+        x_quant(1)
+        w1_turn(1, 0)
+        pre_mm(0, 1, 0)
+        pre_act(0, 0, 1)
+        pre_act(0, 1, 0)
+        x_gain(2)
+        pre_mm(0, 1, 1)
+        pre_prod(0, 0, 0)
+        w1_turn(1, 1)
+        pre_mm(1, 0, 0)
+        pre_act(0, 1, 1)
         x_turn(3)
-        x_gain(3)
-        p_scale(0, 0)
-        pre_prod(0, 1, 2)
+        w1_out(1, 0, False)
         pre_act(1, 0, 0)
-        pre_act(1, 0, 1)
+        pre_prod(0, 0, 1)
         pre_mm(1, 0, 1)
-        pre_prod(1, 0, 0)
-        pre_mm(1, 1, 0)
-        x_quant(3)
-        p_weave_mm(0, 0, 1)
-        pre_act(1, 0, 3)
-        pre_act(1, 0, 2)
-        pre_prod(1, 0, 1)
-        slope(0, 1)
-        pre_prod(1, 0, 3)
-        w1_out(1, 0, True)
-        p_scale(1, 0)
-        pre_prod(1, 0, 2)
+        x_quant(2)
+        slope(0, 0, 0 + 1)
+        pre_prod(0, 1, 0)
+        p_scale(0, 0)
         p_weave_mm(0, 0, 0)
+        w1_out(1, 1, True)
+        pre_mm(1, 1, 0)
+        pre_act(1, 0, 1)
         pre_act(1, 1, 0)
-        pre_act(1, 1, 1)
-        p_weave_out(0, 0, 1)
-        p_scale(0, 1)
+        pre_prod(0, 1, 1)
+        x_gain(3)
         pre_mm(1, 1, 1)
-        pre_prod(1, 1, 0)
-        pre_mm(2, 0, 0)
-        p_weave_mm(1, 0, 1)
-        pre_act(1, 1, 3)
-        pre_act(1, 1, 2)
-        pre_prod(1, 1, 1)
-        p_weave_dve_all(0, 1)
-        slope(1, 0)
-        pre_prod(1, 1, 3)
+        p_weave_mm(0, 0, 1)
+        slope(0, 1, 1 + 1)
+        pre_prod(1, 0, 0)
+        p_scale(0, 1)
         p_weave_out(0, 0, 0)
-        p_scale(2, 0)
-        pre_prod(1, 1, 2)
+        p_scale(1, 0)
         p_weave_mm(1, 0, 0)
-        p_quant(0, 0, 2)
+        pre_mm(2, 0, 0)
+        pre_act(1, 1, 1)
         pre_act(2, 0, 0)
-        pre_act(2, 0, 1)
-        p_weave_out(1, 0, 1)
-        p_scale(1, 1)
+        pre_prod(1, 0, 1)
+        p_weave_out(0, 0, 1)
         pre_mm(2, 0, 1)
-        pre_prod(2, 0, 0)
-        pre_mm(2, 1, 0)
-        p_weave_mm(2, 0, 1)
-        pre_act(2, 0, 3)
-        pre_act(2, 0, 2)
-        pre_prod(2, 0, 1)
-        p_weave_dve_all(1, 1)
-        slope(1, 1)
-        k_mm(0, 0)
-        pre_prod(2, 0, 3)
+        p_weave_mm(1, 0, 1)
+        x_quant(3)
+        slope(1, 0, 0 + 1)
+        pre_prod(1, 1, 0)
+        p_weave_dve_all(0, 1)
+        p_scale(1, 1)
         p_weave_out(1, 0, 0)
-        p_scale(3, 0)
-        pre_prod(2, 0, 2)
-        y_out(0, 0, True)
-        k_mm(0, 1)
+        p_scale(2, 0)
         p_weave_mm(2, 0, 0)
-        y_out(0, 1, True)
-        p_quant(1, 0, 2)
+        pre_mm(2, 1, 0)
+        pre_act(2, 0, 1)
         pre_act(2, 1, 0)
-        pre_act(2, 1, 1)
-        p_weave_out(2, 0, 1)
-        p_scale(2, 1)
-        pre_mm(2, 1, 1)
-        k_mm(0, 2)
-        pre_prod(2, 1, 0)
-        y_out(0, 2, True)
+        pre_prod(1, 1, 1)
+        p_weave_out(1, 0, 1)
+        p_quant(0, 0, 2)
         k_mm(0, 3)
-        pre_mm(3, 0, 0)
+        pre_mm(2, 1, 1)
+        k_mm(0, 0)
+        p_weave_mm(2, 0, 1)
         y_out(0, 3, True)
-        p_weave_mm(3, 0, 1)
-        pre_act(2, 1, 3)
-        pre_act(2, 1, 2)
-        pre_prod(2, 1, 1)
-        p_weave_dve_all(2, 1)
-        slope(2, 0)
-        k_mm(1, 0)
-        pre_prod(2, 1, 3)
-        y_store(0, 0, 2)
+        slope(1, 1, 1 + 1)
+        k_mm(0, 1)
+        pre_prod(2, 0, 0)
+        p_weave_dve_all(1, 1)
+        y_out(0, 0, True)
+        p_scale(2, 1)
+        k_mm(0, 2)
         p_weave_out(2, 0, 0)
-        p_scale(4, 0)
-        pre_prod(2, 1, 2)
-        y_out(1, 0, True)
-        k_mm(1, 1)
+        p_scale(3, 0)
         p_weave_mm(3, 0, 0)
-        y_out(1, 1, True)
-        p_quant(2, 0, 2)
+        pre_mm(3, 0, 0)
+        pre_act(2, 1, 1)
+        y_out(0, 1, True)
         pre_act(3, 0, 0)
-        pre_act(3, 0, 1)
-        p_weave_out(3, 0, 1)
-        p_scale(3, 1)
-        pre_mm(3, 0, 1)
-        k_mm(1, 2)
-        pre_prod(3, 0, 0)
-        y_out(1, 2, True)
+        pre_prod(2, 0, 1)
+        y_out(0, 2, True)
+        p_weave_out(2, 0, 1)
+        p_quant(1, 0, 2)
         k_mm(1, 3)
-        pre_mm(3, 1, 0)
+        pre_mm(3, 0, 1)
+        k_mm(1, 0)
+        p_weave_mm(3, 0, 1)
         y_out(1, 3, True)
-        p_weave_mm(4, 0, 1)
-        pre_act(3, 0, 3)
-        pre_act(3, 0, 2)
-        pre_prod(3, 0, 1)
-        p_weave_dve_all(3, 1)
-        slope(2, 1)
-        k_mm(2, 0)
-        pre_prod(3, 0, 3)
-        y_store(1, 0, 2)
+        slope(2, 0, 0 + 1)
+        k_mm(1, 1)
+        pre_prod(2, 1, 0)
+        p_weave_dve_all(2, 1)
+        y_out(1, 0, True)
+        p_scale(3, 1)
+        k_mm(1, 2)
         p_weave_out(3, 0, 0)
-        p_scale(5, 0)
-        pre_prod(3, 0, 2)
-        y_store(0, 2, 4)
-        y_out(2, 0, True)
-        k_mm(2, 1)
+        p_scale(4, 0)
         p_weave_mm(4, 0, 0)
-        y_out(2, 1, True)
-        p_quant(3, 0, 2)
+        y_store(0, 0, 2)
+        pre_mm(3, 1, 0)
+        pre_act(3, 0, 1)
+        y_out(1, 1, True)
         pre_act(3, 1, 0)
-        pre_act(3, 1, 1)
-        p_weave_out(4, 0, 1)
-        p_scale(4, 1)
-        pre_mm(3, 1, 1)
-        k_mm(2, 2)
-        pre_prod(3, 1, 0)
-        y_out(2, 2, True)
+        pre_prod(2, 1, 1)
+        y_out(1, 2, True)
+        p_weave_out(3, 0, 1)
+        p_quant(2, 0, 2)
         k_mm(2, 3)
-        y_round(0, 2, 4, False)
+        pre_mm(3, 1, 1)
+        k_mm(2, 0)
+        p_weave_mm(4, 0, 1)
         y_out(2, 3, True)
-        p_weave_mm(5, 0, 1)
-        pre_act(3, 1, 3)
-        pre_act(3, 1, 2)
-        pre_prod(3, 1, 1)
-        p_weave_dve_all(4, 1)
-        slope(3, 0)
-        k_mm(3, 0)
-        pre_prod(3, 1, 3)
-        y_store(2, 0, 2)
+        slope(2, 1, 1 + 1)
+        k_mm(2, 1)
+        pre_prod(3, 0, 0)
+        p_weave_dve_all(3, 1)
+        y_out(2, 0, True)
+        p_scale(4, 1)
+        k_mm(2, 2)
         p_weave_out(4, 0, 0)
-        p_scale(6, 0)
-        pre_prod(3, 1, 2)
-        y_store(1, 2, 4)
-        y_round(0, 0, 2, True)
-        y_out(3, 0, True)
-        k_mm(3, 1)
+        p_scale(5, 0)
         p_weave_mm(5, 0, 0)
-        y_out(3, 1, True)
-        p_quant(4, 0, 2)
-        y_turn(0, 1)
-        p_weave_out(5, 0, 1)
+        y_store(1, 0, 2)
+        pre_act(3, 1, 1)
+        y_out(2, 1, True)
+        pre_prod(3, 0, 1)
+        y_out(2, 2, True)
+        p_weave_out(4, 0, 1)
+        p_quant(3, 0, 2)
+        k_mm(3, 3)
+        k_mm(3, 0)
+        p_weave_mm(5, 0, 1)
+        y_out(3, 3, True)
+        y_store(0, 2, 4)
+        slope(3, 0, 0 + 1)
+        k_mm(3, 1)
+        pre_prod(3, 1, 0)
+        p_weave_dve_all(4, 1)
+        y_out(3, 0, True)
         p_scale(5, 1)
         k_mm(3, 2)
-        y_out(3, 2, True)
-        k_mm(3, 3)
-        y_round(1, 2, 4, False)
-        y_out(3, 3, True)
-        p_weave_mm(6, 0, 1)
-        y_turn(0, 0)
-        p_weave_dve_all(5, 1)
-        slope(3, 1)
-        k_mm(4, 0)
-        y_weave(0, 1, True)
-        y_store(3, 0, 2)
         p_weave_out(5, 0, 0)
-        p_scale(7, 0)
-        y_store(2, 2, 4)
-        y_round(1, 0, 2, True)
-        y_out(4, 0, True)
-        k_mm(4, 1)
+        p_scale(6, 0)
         p_weave_mm(6, 0, 0)
-        y_out(4, 1, True)
-        p_quant(5, 0, 2)
-        y_turn(1, 1)
-        y_weave(0, 0, True)
-        p_weave_out(6, 0, 1)
+        y_store(2, 0, 2)
+        y_out(3, 1, True)
+        pre_prod(3, 1, 1)
+        y_out(3, 2, True)
+        p_weave_out(5, 0, 1)
+        p_quant(4, 0, 2)
+        k_mm(4, 3)
+        k_mm(4, 0)
+        p_weave_mm(6, 0, 1)
+        y_round(0, 0, 2, False)
+        y_out(4, 3, True)
+        y_store(1, 2, 4)
+        slope(3, 1, 1 + 1)
+        k_mm(4, 1)
+        p_weave_dve_all(5, 1)
+        y_out(4, 0, True)
         p_scale(6, 1)
         k_mm(4, 2)
-        y_out(4, 2, True)
-        k_mm(4, 3)
-        y_round(2, 2, 4, False)
-        y_out(4, 3, True)
-        p_weave_mm(7, 0, 1)
-        y_turn(1, 0)
-        p_weave_dve_all(6, 1)
-        k_mm(5, 0)
-        y_weave(1, 1, True)
-        y_store(4, 0, 2)
         p_weave_out(6, 0, 0)
-        y_store(3, 2, 4)
-        y_round(2, 0, 2, True)
-        y_out(5, 0, True)
-        k_mm(5, 1)
-        y_quant(0)
+        p_scale(7, 0)
         p_weave_mm(7, 0, 0)
-        y_out(5, 1, True)
-        p_quant(6, 0, 2)
-        y_turn(2, 1)
-        y_weave(1, 0, True)
-        p_weave_out(7, 0, 1)
+        y_round(0, 2, 4, True)
+        y_store(3, 0, 2)
+        y_out(4, 1, True)
+        y_turn(0, 1)
+        y_turn(0, 0)
+        y_out(4, 2, True)
+        p_weave_out(6, 0, 1)
+        p_quant(5, 0, 2)
+        k_mm(5, 3)
+        k_mm(5, 0)
+        p_weave_mm(7, 0, 1)
+        y_weave(0, 1, True)
+        y_out(5, 3, True)
+        y_store(2, 2, 4)
+        k_mm(5, 1)
+        p_weave_dve_all(6, 1)
+        y_out(5, 0, True)
+        y_weave(0, 0, True)
         p_scale(7, 1)
         k_mm(5, 2)
+        p_weave_out(7, 0, 0)
+        y_round(1, 0, 4, False)
+        y_store(4, 0, 2)
+        y_out(5, 1, True)
+        y_turn(1, 1)
+        y_turn(1, 0)
         y_out(5, 2, True)
-        k_mm(5, 3)
-        y_round(3, 0, 4, False)
-        y_out(5, 3, True)
-        y_turn(2, 0)
+        p_weave_out(7, 0, 1)
+        p_quant(6, 0, 2)
+        y_weave(1, 1, True)
+        k_mm(6, 3)
+        y_store(3, 2, 4)
         p_weave_dve_all(7, 1)
         k_mm(6, 0)
-        y_weave(2, 1, True)
+        y_weave(1, 0, True)
+        y_round(2, 0, 4, False)
         y_store(5, 0, 2)
-        p_weave_out(7, 0, 0)
-        y_store(4, 2, 4)
-        y_out(6, 0, False)
-        k_mm(6, 1)
-        y_quant(1)
-        y_out(6, 1, True)
-        y_turn(3, 1)
-        y_weave(2, 0, True)
-        p_quant(7, 0, 2)
-        k_mm(6, 2)
-        y_out(6, 2, True)
-        k_mm(6, 3)
-        y_round(4, 0, 4, False)
         y_out(6, 3, True)
+        y_turn(2, 1)
+        y_turn(2, 0)
+        y_quant(0)
+        y_weave(2, 1, True)
+        y_store(4, 2, 4)
+        y_weave(2, 0, True)
+        y_round(3, 0, 4, False)
+        y_out(6, 0, True)
+        k_mm(6, 1)
+        y_turn(3, 1)
         y_turn(3, 0)
-        k_mm(7, 1)
+        y_quant(1)
         y_weave(3, 1, True)
-        y_store(6, 0, 2)
+        k_mm(6, 2)
         y_store(5, 2, 4)
-        y_quant(2)
-        k_mm(7, 3)
-        k_mm(7, 0)
-        y_turn(4, 1)
         y_weave(3, 0, True)
-        y_out(7, 1, True)
-        y_round(5, 0, 4, False)
-        y_out(7, 3, True)
+        y_out(6, 1, True)
+        y_round(4, 0, 4, False)
+        y_turn(4, 1)
         y_turn(4, 0)
+        y_quant(2)
         y_weave(4, 1, True)
-        y_store(6, 2, 4)
-        y_quant(3)
-        k_mm(7, 2)
-        y_out(7, 0, False)
-        y_turn(5, 1)
         y_weave(4, 0, True)
-        y_round(6, 0, 4, False)
-        y_store(7, 0, 2)
+        p_quant(7, 0, 2)
+        y_round(5, 0, 4, False)
+        y_out(6, 2, False)
+        k_mm(7, 2)
+        y_store(6, 2, 4)
+        y_turn(5, 1)
         y_turn(5, 0)
-        y_out(7, 2, True)
+        y_quant(3)
         y_weave(5, 1, True)
-        y_quant(4)
-        y_store(7, 2, 4)
-        y_turn(6, 1)
         y_weave(5, 0, True)
-        y_round(7, 0, 4, False)
-        y_turn(6, 0)
-        y_weave(6, 1, True)
+        y_quant(4)
+        y_out(7, 2, True)
+        k_mm(7, 0)
+        k_mm(7, 3)
+        y_round(6, 0, 4, False)
+        y_store(6, 0, 2)
         y_quant(5)
         plane_store(0, 6)
-        y_weave(6, 0, True)
-        y_quant(6)
-        y_turn(7, 0)
-        y_weave(7, 0, False)
+        k_mm(7, 1)
+        y_out(7, 3, True)
+        y_out(7, 0, True)
+        y_out(7, 1, False)
+        y_turn(6, 1)
+        y_weave(6, 1, True)
+        y_round(7, 2, 4, False)
+        y_turn(6, 0)
         y_turn(7, 1)
+        y_weave(6, 0, True)
+        y_store(7, 2, 4)
+        y_round(7, 0, 2, False)
+        y_turn(7, 0)
         y_weave(7, 1, True)
+        y_store(7, 0, 2)
+        y_quant(6)
+        y_weave(7, 0, True)
         y_quant(7)
         plane_store(6, 8)

@@ -199,10 +199,11 @@ def tile_linearrelationmeanjacobian_x2_kernel(
 
         def pre_prod(q, g, half):
             silu, tanh = live["st", q, g, half]
+            prod = work.tile([P, 2, 2, N], F32, name="prod", bufs=2 * R)
             for tl in (1, 0):
                 for i in (1, 0):
                     nc.vector.scalar_tensor_tensor(
-                        out=silu[:, tl, i, :],
+                        out=prod[:, tl, i, :],
                         in0=tanh[:, tl, i, :],
                         scalar=1.0,
                         in1=silu[:, tl, i, :],
@@ -301,7 +302,7 @@ def tile_linearrelationmeanjacobian_x2_kernel(
 
         def y_out(r, j, on_scalar):
             if ("y", r) not in live:
-                live["y", r] = work.tile([P, PACK, O], F32, name="y", bufs=R)
+                live["y", r] = work.tile([P, PACK, O], F32, name="y", bufs=4)
             y = live["y", r]
             gain = out_gain[:, r, j : j + 1]
             if on_scalar:
@@ -318,18 +319,19 @@ def tile_linearrelationmeanjacobian_x2_kernel(
         def y_round(r, j0, j1, on_scalar):
             if ("y_bf", r) not in live:
                 live["y_bf", r] = work.tile([P, PACK, O], BF16, name="y_bf", bufs=3)
-            y_bf = live["y_bf", r]
+            dst = live["y_bf", r][:, j0:j1, :].rearrange("p j (u m e) -> p j u m e", u=2, e=2)
+            src = live["y", r][:, j0:j1, :].rearrange("p j (m u e) -> p j u m e", u=2, e=2)
             if on_scalar:
-                nc.scalar.copy(out=y_bf[:, j0:j1, :], in_=live["y", r][:, j0:j1, :])
+                nc.scalar.copy(out=dst, in_=src)
             else:
-                nc.vector.tensor_copy(out=y_bf[:, j0:j1, :], in_=live["y", r][:, j0:j1, :])
+                nc.vector.tensor_copy(out=dst, in_=src)
 
         def y_turn(r, half):
             bank = psum.tile([P, 2, 2, P], F32, name="y_bank", tag="pre" if r >= LATE and half == 1 else "turn")
             words = live["y_bf", r][:, 2 * half : 2 * half + 2, :].bitcast(F32)
             for jl in range(2):
                 for u in range(2):
-                    nc.tensor.transpose(bank[:, jl, u, :], words[:, jl, u : O // 2 : 2], ident_f32[:])
+                    nc.tensor.transpose(bank[:, jl, u, :], words[:, jl, u * P : (u + 1) * P], ident_f32[:])
             live["y_bank", r, half] = bank
 
         def y_weave(r, half, on_scalar):
@@ -365,285 +367,289 @@ def tile_linearrelationmeanjacobian_x2_kernel(
 
 
         loads()
-        small_act()
         consts()
-        w1_turn(0, 0)
-        w1_group(0, 0, 2, False)
-        w1_out(0, 0, True)
-        w1_group(1, 0, 2, True)
-        x_turn(0)
-        w1_turn(0, 1)
-        w1_group(0, 2, 4, False)
-        w1_quant(0, 0, 2)
-        w1_quant(0, 2, 4)
-        x_gain(0)
-        x_turn(1)
         small_dve()
+        w1_group(0, 0, 2, False)
+        w1_group(0, 2, 4, False)
+        x_turn(0)
+        w1_quant(0, 0, 2)
+        small_act()
+        x_gain(0)
+        w1_quant(0, 2, 4)
         x_quant(0)
+        w1_turn(0, 0)
+        w1_group(1, 0, 2, False)
         w1_group(1, 2, 4, False)
+        w1_out(0, 0, True)
+        x_turn(1)
         x_gain(1)
-        w1_quant(1, 0, 4)
-        w1_out(0, 1, True)
         pre_mm(0, 0, 0)
-        x_turn(2)
+        w1_quant(1, 0, 4)
         pre_act(0, 0, 0)
         pre_mm(0, 0, 1)
+        w1_turn(0, 1)
         x_quant(1)
-        w1_turn(1, 0)
-        pre_mm(0, 1, 0)
         pre_act(0, 0, 1)
+        w1_out(0, 1, False)
+        x_turn(2)
+        pre_mm(0, 1, 0)
         pre_act(0, 1, 0)
-        x_gain(2)
-        pre_mm(0, 1, 1)
         pre_prod(0, 0, 0)
-        w1_turn(1, 1)
-        pre_mm(1, 0, 0)
+        w1_turn(1, 0)
+        pre_mm(0, 1, 1)
         pre_act(0, 1, 1)
-        x_turn(3)
+        x_gain(2)
+        pre_prod(0, 0, 1)
+        pre_mm(1, 0, 0)
         w1_out(1, 0, False)
         pre_act(1, 0, 0)
-        pre_prod(0, 0, 1)
+        slope(0, 0, 0 + 1)
+        w1_turn(1, 1)
+        pre_prod(0, 1, 0)
         pre_mm(1, 0, 1)
         x_quant(2)
-        slope(0, 0, 0 + 1)
-        pre_prod(0, 1, 0)
-        p_scale(0, 0)
-        p_weave_mm(0, 0, 0)
-        w1_out(1, 1, True)
-        pre_mm(1, 1, 0)
         pre_act(1, 0, 1)
-        pre_act(1, 1, 0)
         pre_prod(0, 1, 1)
-        x_gain(3)
-        pre_mm(1, 1, 1)
-        p_weave_mm(0, 0, 1)
+        w1_out(1, 1, True)
+        p_scale(0, 0)
+        x_turn(3)
+        pre_mm(1, 1, 0)
+        pre_act(1, 1, 0)
         slope(0, 1, 1 + 1)
         pre_prod(1, 0, 0)
-        p_scale(0, 1)
+        pre_mm(1, 1, 1)
+        p_weave_mm(0, 0, 0)
+        p_weave_mm(0, 0, 1)
         p_weave_out(0, 0, 0)
-        p_scale(1, 0)
-        p_weave_mm(1, 0, 0)
-        pre_mm(2, 0, 0)
         pre_act(1, 1, 1)
-        pre_act(2, 0, 0)
+        x_gain(3)
+        p_scale(0, 1)
         pre_prod(1, 0, 1)
+        p_scale(1, 0)
+        pre_mm(2, 0, 0)
         p_weave_out(0, 0, 1)
-        pre_mm(2, 0, 1)
-        p_weave_mm(1, 0, 1)
-        x_quant(3)
+        pre_act(2, 0, 0)
         slope(1, 0, 0 + 1)
-        pre_prod(1, 1, 0)
         p_weave_dve_all(0, 1)
-        p_scale(1, 1)
+        pre_prod(1, 1, 0)
+        pre_mm(2, 0, 1)
+        p_weave_mm(1, 0, 0)
+        p_weave_mm(1, 0, 1)
         p_weave_out(1, 0, 0)
-        p_scale(2, 0)
-        p_weave_mm(2, 0, 0)
-        pre_mm(2, 1, 0)
+        x_quant(3)
         pre_act(2, 0, 1)
-        pre_act(2, 1, 0)
-        pre_prod(1, 1, 1)
-        p_weave_out(1, 0, 1)
         p_quant(0, 0, 2)
-        k_mm(0, 3)
-        pre_mm(2, 1, 1)
-        k_mm(0, 0)
-        p_weave_mm(2, 0, 1)
-        y_out(0, 3, True)
-        slope(1, 1, 1 + 1)
+        p_scale(1, 1)
         k_mm(0, 1)
-        pre_prod(2, 0, 0)
-        p_weave_dve_all(1, 1)
-        y_out(0, 0, True)
-        p_scale(2, 1)
-        k_mm(0, 2)
-        p_weave_out(2, 0, 0)
-        p_scale(3, 0)
-        p_weave_mm(3, 0, 0)
-        pre_mm(3, 0, 0)
-        pre_act(2, 1, 1)
+        pre_prod(1, 1, 1)
+        p_scale(2, 0)
+        pre_mm(2, 1, 0)
         y_out(0, 1, True)
-        pre_act(3, 0, 0)
-        pre_prod(2, 0, 1)
+        p_weave_out(1, 0, 1)
+        k_mm(0, 0)
+        y_out(0, 0, True)
+        pre_act(2, 1, 0)
+        slope(1, 1, 1 + 1)
+        p_weave_dve_all(1, 1)
+        pre_prod(2, 0, 0)
+        pre_mm(2, 1, 1)
+        p_weave_mm(2, 0, 0)
+        k_mm(0, 3)
+        k_mm(0, 2)
+        y_out(0, 3, True)
+        p_weave_mm(2, 0, 1)
+        p_weave_out(2, 0, 0)
         y_out(0, 2, True)
-        p_weave_out(2, 0, 1)
+        pre_act(2, 1, 1)
         p_quant(1, 0, 2)
-        k_mm(1, 3)
-        pre_mm(3, 0, 1)
-        k_mm(1, 0)
-        p_weave_mm(3, 0, 1)
-        y_out(1, 3, True)
-        slope(2, 0, 0 + 1)
+        p_scale(2, 1)
         k_mm(1, 1)
-        pre_prod(2, 1, 0)
-        p_weave_dve_all(2, 1)
-        y_out(1, 0, True)
-        p_scale(3, 1)
-        k_mm(1, 2)
-        p_weave_out(3, 0, 0)
-        p_scale(4, 0)
-        p_weave_mm(4, 0, 0)
-        y_store(0, 0, 2)
-        pre_mm(3, 1, 0)
-        pre_act(3, 0, 1)
+        pre_prod(2, 0, 1)
+        p_scale(3, 0)
+        pre_mm(3, 0, 0)
         y_out(1, 1, True)
-        pre_act(3, 1, 0)
-        pre_prod(2, 1, 1)
+        p_weave_out(2, 0, 1)
+        y_store(0, 0, 2)
+        k_mm(1, 0)
+        y_out(1, 0, True)
+        pre_act(3, 0, 0)
+        slope(2, 0, 0 + 1)
+        p_weave_dve_all(2, 1)
+        pre_prod(2, 1, 0)
+        pre_mm(3, 0, 1)
+        p_weave_mm(3, 0, 0)
+        k_mm(1, 3)
+        k_mm(1, 2)
+        y_out(1, 3, True)
+        p_weave_mm(3, 0, 1)
+        p_weave_out(3, 0, 0)
         y_out(1, 2, True)
-        p_weave_out(3, 0, 1)
+        pre_act(3, 0, 1)
         p_quant(2, 0, 2)
-        k_mm(2, 3)
-        pre_mm(3, 1, 1)
-        k_mm(2, 0)
-        p_weave_mm(4, 0, 1)
-        y_out(2, 3, True)
-        slope(2, 1, 1 + 1)
+        p_scale(3, 1)
         k_mm(2, 1)
-        pre_prod(3, 0, 0)
-        p_weave_dve_all(3, 1)
-        y_out(2, 0, True)
-        p_scale(4, 1)
-        k_mm(2, 2)
-        p_weave_out(4, 0, 0)
-        p_scale(5, 0)
-        p_weave_mm(5, 0, 0)
-        y_store(1, 0, 2)
-        pre_act(3, 1, 1)
-        y_out(2, 1, True)
-        pre_prod(3, 0, 1)
-        y_out(2, 2, True)
-        p_weave_out(4, 0, 1)
-        p_quant(3, 0, 2)
-        k_mm(3, 3)
-        k_mm(3, 0)
-        p_weave_mm(5, 0, 1)
-        y_out(3, 3, True)
+        pre_prod(2, 1, 1)
+        p_scale(4, 0)
         y_store(0, 2, 4)
-        slope(3, 0, 0 + 1)
+        pre_mm(3, 1, 0)
+        y_out(2, 1, True)
+        p_weave_out(3, 0, 1)
+        y_store(1, 0, 2)
+        k_mm(2, 0)
+        y_out(2, 0, True)
+        pre_act(3, 1, 0)
+        slope(2, 1, 1 + 1)
+        p_weave_dve_all(3, 1)
+        pre_prod(3, 0, 0)
+        pre_mm(3, 1, 1)
+        p_weave_mm(4, 0, 0)
+        y_round(0, 0, 4, False)
+        k_mm(2, 3)
+        k_mm(2, 2)
+        y_out(2, 3, True)
+        p_weave_mm(4, 0, 1)
+        p_weave_out(4, 0, 0)
+        y_out(2, 2, True)
+        pre_act(3, 1, 1)
+        p_quant(3, 0, 2)
+        p_scale(4, 1)
         k_mm(3, 1)
-        pre_prod(3, 1, 0)
-        p_weave_dve_all(4, 1)
-        y_out(3, 0, True)
-        p_scale(5, 1)
-        k_mm(3, 2)
-        p_weave_out(5, 0, 0)
-        p_scale(6, 0)
-        p_weave_mm(6, 0, 0)
-        y_store(2, 0, 2)
-        y_out(3, 1, True)
-        pre_prod(3, 1, 1)
-        y_out(3, 2, True)
-        p_weave_out(5, 0, 1)
-        p_quant(4, 0, 2)
-        k_mm(4, 3)
-        k_mm(4, 0)
-        p_weave_mm(6, 0, 1)
-        y_round(0, 0, 2, False)
-        y_out(4, 3, True)
+        pre_prod(3, 0, 1)
+        p_scale(5, 0)
         y_store(1, 2, 4)
-        slope(3, 1, 1 + 1)
-        k_mm(4, 1)
-        p_weave_dve_all(5, 1)
-        y_out(4, 0, True)
-        p_scale(6, 1)
-        k_mm(4, 2)
-        p_weave_out(6, 0, 0)
-        p_scale(7, 0)
-        p_weave_mm(7, 0, 0)
-        y_round(0, 2, 4, True)
-        y_store(3, 0, 2)
-        y_out(4, 1, True)
+        y_out(3, 1, True)
+        p_weave_out(4, 0, 1)
         y_turn(0, 1)
+        y_store(2, 0, 2)
+        k_mm(3, 0)
+        y_out(3, 0, True)
+        slope(3, 0, 0 + 1)
+        p_weave_dve_all(4, 1)
+        pre_prod(3, 1, 0)
+        p_weave_mm(5, 0, 0)
         y_turn(0, 0)
-        y_out(4, 2, True)
-        p_weave_out(6, 0, 1)
-        p_quant(5, 0, 2)
-        k_mm(5, 3)
-        k_mm(5, 0)
-        p_weave_mm(7, 0, 1)
         y_weave(0, 1, True)
-        y_out(5, 3, True)
-        y_store(2, 2, 4)
-        k_mm(5, 1)
-        p_weave_dve_all(6, 1)
-        y_out(5, 0, True)
+        y_round(1, 2, 4, False)
+        k_mm(3, 3)
+        k_mm(3, 2)
+        y_out(3, 3, True)
+        p_weave_mm(5, 0, 1)
+        p_weave_out(5, 0, 0)
+        y_out(3, 2, True)
+        y_round(1, 0, 2, True)
         y_weave(0, 0, True)
-        p_scale(7, 1)
-        k_mm(5, 2)
-        p_weave_out(7, 0, 0)
-        y_round(1, 0, 4, False)
-        y_store(4, 0, 2)
-        y_out(5, 1, True)
+        p_quant(4, 0, 2)
+        p_scale(5, 1)
+        k_mm(4, 1)
+        pre_prod(3, 1, 1)
+        p_scale(6, 0)
+        y_store(2, 2, 4)
+        y_out(4, 1, True)
+        p_weave_out(5, 0, 1)
         y_turn(1, 1)
+        y_store(3, 0, 2)
+        k_mm(4, 0)
+        y_out(4, 0, True)
+        slope(3, 1, 1 + 1)
+        p_weave_dve_all(5, 1)
+        p_weave_mm(6, 0, 0)
         y_turn(1, 0)
-        y_out(5, 2, True)
-        p_weave_out(7, 0, 1)
-        p_quant(6, 0, 2)
         y_weave(1, 1, True)
-        k_mm(6, 3)
-        y_store(3, 2, 4)
-        p_weave_dve_all(7, 1)
-        k_mm(6, 0)
+        y_round(2, 2, 4, False)
+        k_mm(4, 3)
+        k_mm(4, 2)
+        y_out(4, 3, True)
+        p_weave_mm(6, 0, 1)
+        p_weave_out(6, 0, 0)
+        y_out(4, 2, True)
+        y_round(2, 0, 2, False)
         y_weave(1, 0, True)
-        y_round(2, 0, 4, False)
-        y_store(5, 0, 2)
-        y_out(6, 3, True)
+        p_quant(5, 0, 2)
+        p_scale(6, 1)
+        k_mm(5, 1)
+        p_scale(7, 0)
+        y_store(3, 2, 4)
+        y_out(5, 1, True)
+        p_weave_out(6, 0, 1)
         y_turn(2, 1)
-        y_turn(2, 0)
+        y_store(4, 0, 2)
+        k_mm(5, 0)
+        y_out(5, 0, True)
         y_quant(0)
+        p_weave_dve_all(6, 1)
+        p_weave_mm(7, 0, 0)
+        y_turn(2, 0)
         y_weave(2, 1, True)
-        y_store(4, 2, 4)
+        y_round(3, 2, 4, True)
+        k_mm(5, 3)
+        k_mm(5, 2)
+        y_out(5, 3, True)
+        p_weave_mm(7, 0, 1)
+        p_weave_out(7, 0, 0)
+        y_out(5, 2, True)
+        y_round(3, 0, 2, False)
         y_weave(2, 0, True)
-        y_round(3, 0, 4, False)
-        y_out(6, 0, True)
-        k_mm(6, 1)
+        p_quant(6, 0, 2)
+        p_scale(7, 1)
+        y_store(4, 2, 4)
+        k_mm(6, 3)
+        p_weave_out(7, 0, 1)
         y_turn(3, 1)
-        y_turn(3, 0)
+        y_store(5, 0, 2)
         y_quant(1)
+        p_weave_dve_all(7, 1)
+        y_turn(3, 0)
         y_weave(3, 1, True)
-        k_mm(6, 2)
-        y_store(5, 2, 4)
-        y_weave(3, 0, True)
-        y_out(6, 1, True)
         y_round(4, 0, 4, False)
+        k_mm(6, 2)
+        y_weave(3, 0, True)
+        y_store(5, 2, 4)
         y_turn(4, 1)
-        y_turn(4, 0)
         y_quant(2)
+        y_out(6, 3, False)
+        y_out(6, 2, True)
+        y_turn(4, 0)
         y_weave(4, 1, True)
-        y_weave(4, 0, True)
-        p_quant(7, 0, 2)
         y_round(5, 0, 4, False)
-        y_out(6, 2, False)
-        k_mm(7, 2)
+        k_mm(6, 0)
+        y_weave(4, 0, True)
+        k_mm(6, 1)
         y_store(6, 2, 4)
         y_turn(5, 1)
-        y_turn(5, 0)
+        y_out(6, 0, True)
         y_quant(3)
+        y_out(6, 1, True)
+        p_quant(7, 0, 1)
+        y_turn(5, 0)
+        p_quant(7, 1, 2)
         y_weave(5, 1, True)
-        y_weave(5, 0, True)
-        y_quant(4)
-        y_out(7, 2, True)
-        k_mm(7, 0)
-        k_mm(7, 3)
-        y_round(6, 0, 4, False)
+        y_round(6, 0, 2, False)
         y_store(6, 0, 2)
+        y_weave(5, 0, True)
+        k_mm(7, 0)
+        y_quant(4)
         y_quant(5)
         plane_store(0, 6)
-        k_mm(7, 1)
-        y_out(7, 3, True)
         y_out(7, 0, True)
-        y_out(7, 1, False)
+        y_round(6, 2, 4, False)
+        k_mm(7, 1)
+        k_mm(7, 2)
+        y_out(7, 2, False)
+        y_out(7, 1, True)
+        k_mm(7, 3)
+        y_turn(6, 0)
+        y_store(7, 0, 2)
+        y_out(7, 3, True)
+        y_weave(6, 0, True)
         y_turn(6, 1)
         y_weave(6, 1, True)
-        y_round(7, 2, 4, False)
-        y_turn(6, 0)
-        y_turn(7, 1)
-        y_weave(6, 0, True)
-        y_store(7, 2, 4)
         y_round(7, 0, 2, False)
         y_turn(7, 0)
-        y_weave(7, 1, True)
-        y_store(7, 0, 2)
-        y_quant(6)
         y_weave(7, 0, True)
+        y_round(7, 2, 4, False)
+        y_turn(7, 1)
+        y_store(7, 2, 4)
+        y_weave(7, 1, True)
+        y_quant(6)
         y_quant(7)
         plane_store(6, 8)

@@ -20,7 +20,12 @@ PACK = 4
 K_PASS = P * PACK
 G = H // K_PASS
 PAIRS = R // 2
-LATE = 8
+QUADRANTS = 4
+LAST = R - 1
+
+G_TENSOR, G_VECTOR = 0, 1
+SCALAR_ROUNDS = 2
+PLANE_SPLIT = 4
 
 
 def tile_linearrelationmeanjacobian_x2_kernel(
@@ -61,41 +66,46 @@ def tile_linearrelationmeanjacobian_x2_kernel(
         out_plane = keep.tile([P, R * D], U8, name="out_plane", align_bytes=64)
         live = {}
 
-        def loads():
-            nc.scalar.dma_start(out=gin_bf[:], in_=gin.rearrange("(p t) -> p t", t=PACK))
+        def copy(on_scalar, out, in_):
+            if on_scalar:
+                nc.scalar.copy(out=out, in_=in_)
+            else:
+                nc.vector.tensor_copy(out=out, in_=in_)
+
+        def load_inputs():
+            nc.sync.dma_start(out=gin_bf[:], in_=gin.rearrange("(p t) -> p t", t=PACK))
+            nc.sync.dma_start(out=x_raw[0][:], in_=x[0:2].rearrange("r n d -> n r d"))
             nc.scalar.dma_start(out=b1_bf[:], in_=b1.rearrange("(g p t) -> p g t", g=G, t=PACK))
             nc.scalar.dma_start(out=gamma_bf[:], in_=gamma.rearrange("(g p t) -> p g t", g=G, t=PACK))
-            nc.scalar.dma_start(out=beta_bf[:], in_=beta.partition_broadcast(P))
             for g in range(G):
                 cols = w1[:, g * K_PASS : (g + 1) * K_PASS]
                 nc.sync.dma_start(out=w1_raw[g][:], in_=cols.rearrange("(p j) h -> p j h", j=PACK))
-                if g == 0:
-                    nc.sync.dma_start(out=x_raw[0][:], in_=x[0:2].rearrange("r n d -> n r d"))
             for q in range(1, PAIRS):
                 nc.sync.dma_start(out=x_raw[q][:], in_=x[2 * q : 2 * q + 2].rearrange("r n d -> n r d"))
             nc.sync.dma_start(
                 out=w2_codes[:].bitcast(I32),
                 in_=w2_words.rearrange("g p n t -> p g (n t)").bitcast(I32),
             )
+            nc.sync.dma_start(out=beta_bf[:], in_=beta.partition_broadcast(P))
 
-        def consts():
+        def set_up():
             make_identity(nc, ident_f32[:])
             nc.vector.memset(warm[:], 0.0)
             nc.scalar.activation(out=warm_out[:], in_=warm[:], func=ACT.Silu)
             make_identity(nc, ident_bf[:])
             nc.gpsimd.memset(w2_plane[:].bitcast(I32), 0)
-            for quad in range(4):
+            for quad in range(QUADRANTS):
                 nc.sync.dma_start(
                     out=w2_plane[32 * quad : 32 * quad + 4].bitcast(I32),
                     in_=w2_scales[:, 4 * quad : 4 * quad + 4, :].rearrange("g q n -> q g n").bitcast(I32),
                 )
 
-        def small_act():
+        def hidden_constants():
             nc.scalar.activation(out=b1_half[:], in_=b1_bf[:], func=ACT.Copy, scale=0.5)
             nc.scalar.activation(out=b1_full[:], in_=b1_bf[:], func=ACT.Copy)
             nc.scalar.activation(out=gamma_n[:], in_=gamma_bf[:], func=ACT.Copy, scale=0.5 / N)
 
-        def small_dve():
+        def output_gain():
             nc.vector.tensor_tensor(
                 out=out_gain[:],
                 in0=beta_bf[:].unsqueeze(2).to_broadcast([P, R, PACK]),
@@ -103,18 +113,18 @@ def tile_linearrelationmeanjacobian_x2_kernel(
                 op=ALU.mult,
             )
 
-        def x_turn(q):
+
+        def x_transpose(q):
             bank = psum.tile([P, 2, 2, N], F32, name="x_bank", tag="turn")
-            words = x_raw[q][:].bitcast(F32)
+            pairs = x_raw[q][:].bitcast(F32)
             for i in range(2):
                 for u in range(2):
-                    nc.tensor.transpose(bank[:, u, i, :], words[:, i, u : D // 2 : 2], ident_f32[:])
+                    nc.tensor.transpose(bank[:, u, i, :], pairs[:, i, u : D // 2 : 2], ident_f32[:])
             live["x_bank", q] = bank
 
         def x_gain(q):
-            bank = live["x_bank", q]
             xg = work.tile([P, 2 * N, 2, 2], BF16, name="xg", align_bytes=64)
-            src = bank[:].rearrange("p u i n -> p (u i n)").bitcast(BF16)
+            src = live["x_bank", q][:].rearrange("p u i n -> p (u i n)").bitcast(BF16)
             nc.vector.tensor_tensor(
                 out=xg[:],
                 in0=src.rearrange("p (u m e) -> p m u e", u=2, e=2),
@@ -123,43 +133,39 @@ def tile_linearrelationmeanjacobian_x2_kernel(
             )
             live["xg", q] = xg
 
-        def x_quant(q):
+        def x_quantize(q):
             nc.vector.quantize_mx(
                 out=x_codes[q][:].bitcast(FP8X4),
                 scales=x_scales[q][:],
                 in_=live["xg", q][:].rearrange("p m u e -> p (m u e)"),
             )
 
-        def w1_group(g, t0, t1, on_scalar):
-            src = w1_raw[g][:].rearrange("p j (m t) -> p t m j", t=PACK)[:, t0:t1]
-            if on_scalar:
-                nc.scalar.copy(out=w1_grouped[g][:, t0:t1], in_=src)
-            else:
-                nc.vector.tensor_copy(out=w1_grouped[g][:, t0:t1], in_=src)
+        def w1_interleave(g, half, on_scalar):
+            ts = slice(2 * half, 2 * half + 2)
+            copy(on_scalar, w1_grouped[g][:, ts], w1_raw[g][:].rearrange("p j (m t) -> p t m j", t=PACK)[:, ts])
 
-        def w1_quant(g, t0, t1):
+        def w1_quantize(g, t0, t1):
             nc.vector.quantize_mx(
                 out=w1_codes[g][:, t0 * P : t1 * P].bitcast(FP8X4),
                 scales=w1_scales[g][:, t0 * P : t1 * P],
                 in_=w1_grouped[g][:, t0:t1].rearrange("p t m j -> p (t m j)"),
             )
 
-        def w1_turn(g, half):
+        def w1_transpose(g, half):
             bank = psum.tile([P, 2, PACK, P], BF16, name="w1_bank", tag="weave")
             for tl in range(2):
                 for j in range(PACK):
-                    nc.tensor.transpose(bank[:, tl, j, :], w1_raw[g][:, j, 2 * half + tl : K_PASS : PACK], ident_bf[:])
+                    src = w1_raw[g][:, j, 2 * half + tl : K_PASS : PACK]
+                    nc.tensor.transpose(bank[:, tl, j, :], src, ident_bf[:])
             live["w1_bank", g, half] = bank
 
-        def w1_out(g, half, on_scalar):
-            src = live["w1_bank", g, half][:].rearrange("p t j c -> p (t j c)")
+        def w1_copy_out(g, half, on_scalar):
             dst = w1_t[g][:, 2 * half : 2 * half + 2].rearrange("p t d -> p (t d)")
-            if on_scalar:
-                nc.scalar.copy(out=dst, in_=src)
-            else:
-                nc.vector.tensor_copy(out=dst, in_=src)
+            copy(on_scalar, dst, live["w1_bank", g, half][:].rearrange("p t j c -> p (t j c)"))
 
-        def pre_mm(q, g, half):
+
+        def hidden_matmul(s, half):
+            q, g = divmod(s, G)
             bank = psum.tile([P, 2, 2 * N], F32, name="pre_bank", tag="pre")
             for tl in range(2):
                 cols = slice((2 * half + tl) * P, (2 * half + tl + 1) * P)
@@ -172,10 +178,11 @@ def tile_linearrelationmeanjacobian_x2_kernel(
                     start=True,
                     stop=True,
                 )
-            live["pre", q, g, half] = bank
+            live["pre", s, half] = bank
 
-        def pre_act(q, g, half):
-            bank = live["pre", q, g, half]
+        def hidden_activations(s, half):
+            q, g = divmod(s, G)
+            bank = live["pre", s, half]
             silu = work.tile([P, 2, 2, N], F32, name="silu", bufs=4)
             tanh = work.tile([P, 2, 2, N], F32, name="tanh", bufs=4)
             for tl in range(2):
@@ -195,11 +202,12 @@ def tile_linearrelationmeanjacobian_x2_kernel(
                         scale=0.5,
                         accum_out=tanh_sum[:, q, g, t, i : i + 1],
                     )
-            live["st", q, g, half] = (silu, tanh)
+            live["act", s, half] = (silu, tanh)
 
-        def pre_prod(q, g, half):
-            silu, tanh = live["st", q, g, half]
-            prod = work.tile([P, 2, 2, N], F32, name="prod", bufs=2 * R)
+        def slope_products(s, half):
+            q, g = divmod(s, G)
+            silu, tanh = live["act", s, half]
+            prod = work.tile([P, 2, 2, N], F32, name="prod", bufs=2 * G * PAIRS)
             for tl in (1, 0):
                 for i in (1, 0):
                     nc.vector.scalar_tensor_tensor(
@@ -212,15 +220,16 @@ def tile_linearrelationmeanjacobian_x2_kernel(
                         accum_out=prod_sum[:, q, g, 2 * half + tl, i : i + 1],
                     )
 
-        def slope(q, g0, g1):
+        def slope_sums(q):
             nc.vector.scalar_tensor_tensor(
-                out=slope_sum[:, q, g0:g1].rearrange("p g t i -> p (g t i)"),
-                in0=tanh_sum[:, q, g0:g1].rearrange("p g t i -> p (g t i)"),
+                out=slope_sum[:, q].rearrange("p g t i -> p (g t i)"),
+                in0=tanh_sum[:, q].rearrange("p g t i -> p (g t i)"),
                 scalar=float(N),
-                in1=prod_sum[:, q, g0:g1].rearrange("p g t i -> p (g t i)"),
+                in1=prod_sum[:, q].rearrange("p g t i -> p (g t i)"),
                 op0=ALU.add,
                 op1=ALU.subtract,
             )
+
 
         def p_scale(r, g):
             rows = work.tile([P, PACK, D], BF16, name="p_rows", bufs=3)
@@ -235,60 +244,53 @@ def tile_linearrelationmeanjacobian_x2_kernel(
                 )
             live["rows", r, g] = rows
 
-        def grouped(r, g):
+        def p_grouped(r):
             if ("grouped", r) not in live:
                 live["grouped", r] = work.tile([P, G, D, PACK], BF16, name="p_grouped", bufs=3, align_bytes=64)
-            return live["grouped", r][:, g]
+            return live["grouped", r]
 
-        def p_weave_dve(r, g, half):
-            cols = slice(half * 256, (half + 1) * 256)
+        def p_interleave_vector(r):
             nc.vector.tensor_copy(
-                out=grouped(r, g)[:, cols, :].rearrange("p (c i) t -> p c t i", i=4),
-                in_=live["rows", r, g][:, :, cols].rearrange("p t (c i) -> p c t i", i=4),
+                out=p_grouped(r)[:, G_VECTOR].rearrange("p (c i) t -> p c t i", i=4),
+                in_=live["rows", r, G_VECTOR][:].rearrange("p t (c i) -> p c t i", i=4),
             )
 
-        def p_weave_dve_all(r, g):
-            nc.vector.tensor_copy(
-                out=grouped(r, g)[:].rearrange("p (c i) t -> p c t i", i=4),
-                in_=live["rows", r, g][:].rearrange("p t (c i) -> p c t i", i=4),
-            )
-
-        def p_weave_mm(r, g, half):
+        def p_interleave_tensor(r, half):
             bank = psum.tile([P, 2, P, PACK], BF16, name="weave_bank", tag="weave")
-            for s in range(2):
-                d0 = (2 * half + s) * P
+            for part in range(2):
+                d0 = (2 * half + part) * P
                 nc.tensor.matmul(
-                    bank[:, s].rearrange("p d t -> p (d t)"),
+                    bank[:, part].rearrange("p d t -> p (d t)"),
                     lhsT=ident_bf[:],
-                    rhs=live["rows", r, g][:, :, d0 : d0 + P].rearrange("p t d -> p d t"),
+                    rhs=live["rows", r, G_TENSOR][:, :, d0 : d0 + P].rearrange("p t d -> p d t"),
                     start=True,
                     stop=True,
                 )
-            live["weave", r, g, half] = bank
+            live["weave", r, half] = bank
 
-        def p_weave_out(r, g, half):
+        def p_copy_out(r, half):
+            cols = slice(half * D // 2, (half + 1) * D // 2)
             nc.scalar.copy(
-                out=grouped(r, g)[:, half * 256 : (half + 1) * 256, :].rearrange("p d t -> p (d t)"),
-                in_=live["weave", r, g, half][:].rearrange("p s d t -> p (s d t)"),
+                out=p_grouped(r)[:, G_TENSOR, cols, :].rearrange("p d t -> p (d t)"),
+                in_=live["weave", r, half][:].rearrange("p s d t -> p (s d t)"),
             )
 
-        def p_quant(r, g0, g1):
-            if ("p", r) not in live:
-                codes = work.tile([P, G, D], U32, name="p_codes", bufs=3, align_bytes=64)
-                scales = work.tile([P, G, D], U8, name="p_scales", bufs=3, align_bytes=64)
-                live["p", r] = (codes, scales)
-            codes, scales = live["p", r]
+        def p_quantize(r):
+            codes = work.tile([P, G, D], U32, name="p_codes", bufs=3, align_bytes=64)
+            scales = work.tile([P, G, D], U8, name="p_scales", bufs=3, align_bytes=64)
             nc.vector.quantize_mx(
-                out=codes[:, g0:g1].rearrange("p g d -> p (g d)").bitcast(FP8X4),
-                scales=scales[:, g0:g1].rearrange("p g d -> p (g d)"),
-                in_=live["grouped", r][:, g0:g1].rearrange("p g d t -> p (g d t)"),
+                out=codes[:].rearrange("p g d -> p (g d)").bitcast(FP8X4),
+                scales=scales[:].rearrange("p g d -> p (g d)"),
+                in_=p_grouped(r)[:].rearrange("p g d t -> p (g d t)"),
             )
+            live["p", r] = (codes, scales)
 
-        def k_mm(r, j):
-            bank = psum.tile([P, O], F32, name="k_bank", tag="weave" if r == R - 1 and j >= 2 else "k")
+
+        def out_matmul(r, j):
+            bank = psum.tile([P, O], F32, name="k_bank", tag="weave" if r == LAST and j >= 2 else "k")
             cols = slice(j * P, (j + 1) * P)
+            codes, scales = live["p", r]
             for g in range(G):
-                codes, scales = live["p", r]
                 nc.tensor.matmul_mx(
                     out=bank[:],
                     lhsT=codes[:, g, cols].bitcast(FP8X4),
@@ -300,51 +302,45 @@ def tile_linearrelationmeanjacobian_x2_kernel(
                 )
             live["k", r, j] = bank
 
-        def y_out(r, j, on_scalar):
+        def y_copy_out(r, j):
             if ("y", r) not in live:
                 live["y", r] = work.tile([P, PACK, O], F32, name="y", bufs=4)
-            y = live["y", r]
-            gain = out_gain[:, r, j : j + 1]
-            if on_scalar:
-                nc.scalar.activation(out=y[:, j, :], in_=live["k", r, j][:], func=ACT.Copy, scale=gain)
-            else:
-                nc.vector.tensor_scalar(
-                    out=y[:, j, :], in0=live["k", r, j][:], scalar1=gain, scalar2=None, op0=ALU.mult
-                )
+            nc.scalar.activation(
+                out=live["y", r][:, j, :], in_=live["k", r, j][:], func=ACT.Copy, scale=out_gain[:, r, j : j + 1]
+            )
 
-        def y_store(r, j0, j1):
+        def y_store(r, half):
+            js = slice(2 * half, 2 * half + 2)
             rows = out_0[r].rearrange("(c j) o -> c j o", j=PACK)
-            nc.sync.dma_start(out=rows[:, j0:j1, :], in_=live["y", r][:, j0:j1, :])
+            nc.sync.dma_start(out=rows[:, js, :], in_=live["y", r][:, js, :])
 
         def y_round(r, j0, j1, on_scalar):
             if ("y_bf", r) not in live:
                 live["y_bf", r] = work.tile([P, PACK, O], BF16, name="y_bf", bufs=3)
             dst = live["y_bf", r][:, j0:j1, :].rearrange("p j (u m e) -> p j u m e", u=2, e=2)
             src = live["y", r][:, j0:j1, :].rearrange("p j (m u e) -> p j u m e", u=2, e=2)
-            if on_scalar:
-                nc.scalar.copy(out=dst, in_=src)
-            else:
-                nc.vector.tensor_copy(out=dst, in_=src)
+            copy(on_scalar, dst, src)
 
-        def y_turn(r, half):
-            bank = psum.tile([P, 2, 2, P], F32, name="y_bank", tag="pre" if r >= LATE and half == 1 else "turn")
-            words = live["y_bf", r][:, 2 * half : 2 * half + 2, :].bitcast(F32)
+        def y_round_vector(r):
+            y_round(r, 2 if r < SCALAR_ROUNDS else 0, PACK, False)
+
+        def y_transpose(r, half):
+            bank = psum.tile([P, 2, 2, P], F32, name="y_bank", tag="turn")
+            pairs = live["y_bf", r][:, 2 * half : 2 * half + 2, :].bitcast(F32)
             for jl in range(2):
                 for u in range(2):
-                    nc.tensor.transpose(bank[:, jl, u, :], words[:, jl, u * P : (u + 1) * P], ident_f32[:])
+                    nc.tensor.transpose(bank[:, jl, u, :], pairs[:, jl, u * P : (u + 1) * P], ident_f32[:])
             live["y_bank", r, half] = bank
 
-        def y_weave(r, half, on_scalar):
+        def y_interleave(r, half):
             if ("y_grouped", r) not in live:
                 live["y_grouped", r] = work.tile([P, P, PACK, 2], F32, name="y_grouped", bufs=3, align_bytes=64)
-            dst = live["y_grouped", r][:, :, 2 * half : 2 * half + 2, :]
-            src = live["y_bank", r, half][:].rearrange("p j u c -> p c j u")
-            if on_scalar:
-                nc.scalar.copy(out=dst, in_=src)
-            else:
-                nc.vector.tensor_copy(out=dst, in_=src)
+            nc.scalar.copy(
+                out=live["y_grouped", r][:, :, 2 * half : 2 * half + 2, :],
+                in_=live["y_bank", r, half][:].rearrange("p j u c -> p c j u"),
+            )
 
-        def y_quant(r):
+        def y_quantize(r):
             codes = work.tile([P, D], U32, name="y_codes", bufs=R, align_bytes=64)
             cols = slice(r * D, (r + 1) * D)
             nc.vector.quantize_mx(
@@ -356,300 +352,104 @@ def tile_linearrelationmeanjacobian_x2_kernel(
                 out=out_1[0, :, cols, :].rearrange("p m t -> p (m t)").bitcast(I32), in_=codes[:].bitcast(I32)
             )
 
-        def plane_store(r0, r1):
+        def scale_rows_store(queue, r0, r1):
             cols = slice(r0 * D, r1 * D)
-            for quad in range(4):
-                queue = nc.scalar if r1 == R else nc.sync
+            for quad in range(QUADRANTS):
                 queue.dma_start(
                     out=out_2[0, 4 * quad : 4 * quad + 4, cols].bitcast(I32),
                     in_=out_plane[32 * quad : 32 * quad + 4, cols].bitcast(I32),
                 )
 
-
-        loads()
-        consts()
-        small_dve()
-        w1_group(0, 0, 2, False)
-        w1_group(0, 2, 4, False)
-        x_turn(0)
-        w1_quant(0, 0, 2)
-        small_act()
+        load_inputs()
+        set_up()
+        x_transpose(0)
+        w1_interleave(0, 1, True)
+        w1_transpose(0, 1)
         x_gain(0)
-        w1_quant(0, 2, 4)
-        x_quant(0)
-        w1_turn(0, 0)
-        w1_group(1, 0, 2, False)
-        w1_group(1, 2, 4, False)
-        w1_out(0, 0, True)
-        x_turn(1)
+        w1_interleave(1, 0, True)
+        w1_interleave(0, 0, False)
+        w1_quantize(0, 0, 2)
+        w1_quantize(0, 2, PACK)
+        w1_transpose(1, 1)
+        hidden_constants()
+        w1_interleave(1, 1, False)
+        x_quantize(0)
+        w1_quantize(1, 0, PACK)
+        x_transpose(1)
         x_gain(1)
-        pre_mm(0, 0, 0)
-        w1_quant(1, 0, 4)
-        pre_act(0, 0, 0)
-        pre_mm(0, 0, 1)
-        w1_turn(0, 1)
-        x_quant(1)
-        pre_act(0, 0, 1)
-        w1_out(0, 1, False)
-        x_turn(2)
-        pre_mm(0, 1, 0)
-        pre_act(0, 1, 0)
-        pre_prod(0, 0, 0)
-        w1_turn(1, 0)
-        pre_mm(0, 1, 1)
-        pre_act(0, 1, 1)
-        x_gain(2)
-        pre_prod(0, 0, 1)
-        pre_mm(1, 0, 0)
-        w1_out(1, 0, False)
-        pre_act(1, 0, 0)
-        slope(0, 0, 0 + 1)
-        w1_turn(1, 1)
-        pre_prod(0, 1, 0)
-        pre_mm(1, 0, 1)
-        x_quant(2)
-        pre_act(1, 0, 1)
-        pre_prod(0, 1, 1)
-        w1_out(1, 1, True)
-        p_scale(0, 0)
-        x_turn(3)
-        pre_mm(1, 1, 0)
-        pre_act(1, 1, 0)
-        slope(0, 1, 1 + 1)
-        pre_prod(1, 0, 0)
-        pre_mm(1, 1, 1)
-        p_weave_mm(0, 0, 0)
-        p_weave_mm(0, 0, 1)
-        p_weave_out(0, 0, 0)
-        pre_act(1, 1, 1)
-        x_gain(3)
-        p_scale(0, 1)
-        pre_prod(1, 0, 1)
-        p_scale(1, 0)
-        pre_mm(2, 0, 0)
-        p_weave_out(0, 0, 1)
-        pre_act(2, 0, 0)
-        slope(1, 0, 0 + 1)
-        p_weave_dve_all(0, 1)
-        pre_prod(1, 1, 0)
-        pre_mm(2, 0, 1)
-        p_weave_mm(1, 0, 0)
-        p_weave_mm(1, 0, 1)
-        p_weave_out(1, 0, 0)
-        x_quant(3)
-        pre_act(2, 0, 1)
-        p_quant(0, 0, 2)
-        p_scale(1, 1)
-        k_mm(0, 1)
-        pre_prod(1, 1, 1)
-        p_scale(2, 0)
-        pre_mm(2, 1, 0)
-        y_out(0, 1, True)
-        p_weave_out(1, 0, 1)
-        k_mm(0, 0)
-        y_out(0, 0, True)
-        pre_act(2, 1, 0)
-        slope(1, 1, 1 + 1)
-        p_weave_dve_all(1, 1)
-        pre_prod(2, 0, 0)
-        pre_mm(2, 1, 1)
-        p_weave_mm(2, 0, 0)
-        k_mm(0, 3)
-        k_mm(0, 2)
-        y_out(0, 3, True)
-        p_weave_mm(2, 0, 1)
-        p_weave_out(2, 0, 0)
-        y_out(0, 2, True)
-        pre_act(2, 1, 1)
-        p_quant(1, 0, 2)
-        p_scale(2, 1)
-        k_mm(1, 1)
-        pre_prod(2, 0, 1)
-        p_scale(3, 0)
-        pre_mm(3, 0, 0)
-        y_out(1, 1, True)
-        p_weave_out(2, 0, 1)
-        y_store(0, 0, 2)
-        k_mm(1, 0)
-        y_out(1, 0, True)
-        pre_act(3, 0, 0)
-        slope(2, 0, 0 + 1)
-        p_weave_dve_all(2, 1)
-        pre_prod(2, 1, 0)
-        pre_mm(3, 0, 1)
-        p_weave_mm(3, 0, 0)
-        k_mm(1, 3)
-        k_mm(1, 2)
-        y_out(1, 3, True)
-        p_weave_mm(3, 0, 1)
-        p_weave_out(3, 0, 0)
-        y_out(1, 2, True)
-        pre_act(3, 0, 1)
-        p_quant(2, 0, 2)
-        p_scale(3, 1)
-        k_mm(2, 1)
-        pre_prod(2, 1, 1)
-        p_scale(4, 0)
-        y_store(0, 2, 4)
-        pre_mm(3, 1, 0)
-        y_out(2, 1, True)
-        p_weave_out(3, 0, 1)
-        y_store(1, 0, 2)
-        k_mm(2, 0)
-        y_out(2, 0, True)
-        pre_act(3, 1, 0)
-        slope(2, 1, 1 + 1)
-        p_weave_dve_all(3, 1)
-        pre_prod(3, 0, 0)
-        pre_mm(3, 1, 1)
-        p_weave_mm(4, 0, 0)
-        y_round(0, 0, 4, False)
-        k_mm(2, 3)
-        k_mm(2, 2)
-        y_out(2, 3, True)
-        p_weave_mm(4, 0, 1)
-        p_weave_out(4, 0, 0)
-        y_out(2, 2, True)
-        pre_act(3, 1, 1)
-        p_quant(3, 0, 2)
-        p_scale(4, 1)
-        k_mm(3, 1)
-        pre_prod(3, 0, 1)
-        p_scale(5, 0)
-        y_store(1, 2, 4)
-        y_out(3, 1, True)
-        p_weave_out(4, 0, 1)
-        y_turn(0, 1)
-        y_store(2, 0, 2)
-        k_mm(3, 0)
-        y_out(3, 0, True)
-        slope(3, 0, 0 + 1)
-        p_weave_dve_all(4, 1)
-        pre_prod(3, 1, 0)
-        p_weave_mm(5, 0, 0)
-        y_turn(0, 0)
-        y_weave(0, 1, True)
-        y_round(1, 2, 4, False)
-        k_mm(3, 3)
-        k_mm(3, 2)
-        y_out(3, 3, True)
-        p_weave_mm(5, 0, 1)
-        p_weave_out(5, 0, 0)
-        y_out(3, 2, True)
-        y_round(1, 0, 2, True)
-        y_weave(0, 0, True)
-        p_quant(4, 0, 2)
-        p_scale(5, 1)
-        k_mm(4, 1)
-        pre_prod(3, 1, 1)
-        p_scale(6, 0)
-        y_store(2, 2, 4)
-        y_out(4, 1, True)
-        p_weave_out(5, 0, 1)
-        y_turn(1, 1)
-        y_store(3, 0, 2)
-        k_mm(4, 0)
-        y_out(4, 0, True)
-        slope(3, 1, 1 + 1)
-        p_weave_dve_all(5, 1)
-        p_weave_mm(6, 0, 0)
-        y_turn(1, 0)
-        y_weave(1, 1, True)
-        y_round(2, 2, 4, False)
-        k_mm(4, 3)
-        k_mm(4, 2)
-        y_out(4, 3, True)
-        p_weave_mm(6, 0, 1)
-        p_weave_out(6, 0, 0)
-        y_out(4, 2, True)
-        y_round(2, 0, 2, False)
-        y_weave(1, 0, True)
-        p_quant(5, 0, 2)
-        p_scale(6, 1)
-        k_mm(5, 1)
-        p_scale(7, 0)
-        y_store(3, 2, 4)
-        y_out(5, 1, True)
-        p_weave_out(6, 0, 1)
-        y_turn(2, 1)
-        y_store(4, 0, 2)
-        k_mm(5, 0)
-        y_out(5, 0, True)
-        y_quant(0)
-        p_weave_dve_all(6, 1)
-        p_weave_mm(7, 0, 0)
-        y_turn(2, 0)
-        y_weave(2, 1, True)
-        y_round(3, 2, 4, True)
-        k_mm(5, 3)
-        k_mm(5, 2)
-        y_out(5, 3, True)
-        p_weave_mm(7, 0, 1)
-        p_weave_out(7, 0, 0)
-        y_out(5, 2, True)
-        y_round(3, 0, 2, False)
-        y_weave(2, 0, True)
-        p_quant(6, 0, 2)
-        p_scale(7, 1)
-        y_store(4, 2, 4)
-        k_mm(6, 3)
-        p_weave_out(7, 0, 1)
-        y_turn(3, 1)
-        y_store(5, 0, 2)
-        y_quant(1)
-        p_weave_dve_all(7, 1)
-        y_turn(3, 0)
-        y_weave(3, 1, True)
-        y_round(4, 0, 4, False)
-        k_mm(6, 2)
-        y_weave(3, 0, True)
-        y_store(5, 2, 4)
-        y_turn(4, 1)
-        y_quant(2)
-        y_out(6, 3, False)
-        y_out(6, 2, True)
-        y_turn(4, 0)
-        y_weave(4, 1, True)
-        y_round(5, 0, 4, False)
-        k_mm(6, 0)
-        y_weave(4, 0, True)
-        k_mm(6, 1)
-        y_store(6, 2, 4)
-        y_turn(5, 1)
-        y_out(6, 0, True)
-        y_quant(3)
-        y_out(6, 1, True)
-        p_quant(7, 0, 1)
-        y_turn(5, 0)
-        p_quant(7, 1, 2)
-        y_weave(5, 1, True)
-        y_round(6, 0, 2, False)
-        y_store(6, 0, 2)
-        y_weave(5, 0, True)
-        k_mm(7, 0)
-        y_quant(4)
-        y_quant(5)
-        plane_store(0, 6)
-        y_out(7, 0, True)
-        y_round(6, 2, 4, False)
-        k_mm(7, 1)
-        k_mm(7, 2)
-        y_out(7, 2, False)
-        y_out(7, 1, True)
-        k_mm(7, 3)
-        y_turn(6, 0)
-        y_store(7, 0, 2)
-        y_out(7, 3, True)
-        y_weave(6, 0, True)
-        y_turn(6, 1)
-        y_weave(6, 1, True)
-        y_round(7, 0, 2, False)
-        y_turn(7, 0)
-        y_weave(7, 0, True)
-        y_round(7, 2, 4, False)
-        y_turn(7, 1)
-        y_store(7, 2, 4)
-        y_weave(7, 1, True)
-        y_quant(6)
-        y_quant(7)
-        plane_store(6, 8)
+        x_quantize(1)
+        w1_copy_out(1, 1, True)
+
+        units = range(G * PAIRS)
+        relations = range(R)
+        steady = range(LAST)
+        once = (0,)
+        last = (LAST,)
+        timetable = [
+            (5, relations, lambda r: p_copy_out(r, 0)),
+            (6, steady, lambda r: y_copy_out(r, 2)),
+            (6, last, lambda r: y_copy_out(r, 3)),
+            (4, relations, lambda r: p_scale(r, G_TENSOR)),
+            (5, relations, p_interleave_vector),
+            (-3, units[2 * G :: G], lambda s: x_gain(s // G)),
+            (1, units, lambda s: hidden_activations(s, 1)),
+            (9, steady, lambda r: y_interleave(r, 1)),
+            (9, steady, lambda r: y_transpose(r, 0)),
+            (2, once, lambda i: w1_copy_out(0, 0, False)),
+            (2, units, lambda s: slope_products(s, 1)),
+            (4, relations, lambda r: p_interleave_tensor(r, 1)),
+            (5, once, lambda i: output_gain()),
+            (6, steady, lambda r: out_matmul(r, 3)),
+            (6, steady, lambda r: out_matmul(r, 0)),
+            (7, last, lambda r: out_matmul(r, 1)),
+            (0, once, lambda i: w1_copy_out(0, 1, True)),
+            (11, range(LAST - 2), y_quantize),
+            (11 + PLANE_SPLIT - 1, once, lambda i: scale_rows_store(nc.sync, 0, PLANE_SPLIT)),
+            (-3, units[2 * G :: G], lambda s: x_quantize(s // G)),
+            (5, relations, p_quantize),
+            (0, units, lambda s: hidden_matmul(s, 0)),
+            (4, relations, lambda r: p_scale(r, G_VECTOR)),
+            (5, last, lambda r: out_matmul(r, 2)),
+            (6, steady, lambda r: y_copy_out(r, 3)),
+            (4, relations, lambda r: p_interleave_tensor(r, 0)),
+            (-4, units[2 * G :: G], lambda s: x_transpose(s // G)),
+            (9, steady, lambda r: y_interleave(r, 0)),
+            (6, steady, lambda r: y_copy_out(r, 0)),
+            (5, last, lambda r: out_matmul(r, 3)),
+            (5, last, lambda r: y_copy_out(r, 2)),
+            (2, units[1::G], lambda s: slope_sums(s // G)),
+            (6, last, lambda r: y_store(r, 1)),
+            (1, once, lambda i: w1_transpose(1, 0)),
+            (0, units, lambda s: hidden_activations(s, 0)),
+            (6, steady, lambda r: y_store(r, 1)),
+            (5, steady, lambda r: out_matmul(r, 1)),
+            (0, units, lambda s: hidden_matmul(s, 1)),
+            (8, steady, y_round_vector),
+            (0, once, lambda i: w1_transpose(0, 0)),
+            (6, last, lambda r: out_matmul(r, 0)),
+            (5, steady, lambda r: out_matmul(r, 2)),
+            (8, range(SCALAR_ROUNDS), lambda r: y_round(r, 0, 2, True)),
+            (6, steady, lambda r: y_store(r, 0)),
+            (8, steady, lambda r: y_transpose(r, 1)),
+            (6, last, lambda r: y_copy_out(r, 0)),
+            (7, last, lambda r: y_copy_out(r, 1)),
+            (2, once, lambda i: w1_copy_out(1, 0, False)),
+            (4, relations, lambda r: p_copy_out(r, 1)),
+            (1, units, lambda s: slope_products(s, 0)),
+            (5, steady, lambda r: y_copy_out(r, 1)),
+        ]
+        for slot in range(2 * R):
+            for first, indices, step in timetable:
+                if slot - first in indices:
+                    step(slot - first)
+
+        y_store(LAST, 0)
+        y_round(LAST, 2, PACK, False)
+        y_quantize(LAST - 2)
+        y_round(LAST, 0, 2, False)
+        y_quantize(LAST - 1)
+        for half in (1, 0):
+            y_transpose(LAST, half)
+            y_interleave(LAST, half)
+        y_quantize(LAST)
+        scale_rows_store(nc.scalar, PLANE_SPLIT, R)

from contextlib import ExitStack

import concourse.mybir as mybir
from concourse.masks import make_identity

R, N, D, H, O = 8, 128, 512, 1024, 512
FLOPS = 2 * R * N * D * H + 2 * R * D * H * O

F32 = mybir.dt.float32
BF16 = mybir.dt.bfloat16
U32 = mybir.dt.uint32
I32 = mybir.dt.int32
U8 = mybir.dt.uint8
FP8X4 = mybir.dt.float8_e4m3fn_x4
ALU = mybir.AluOpType
ACT = mybir.ActivationFunctionType

P = 128
PACK = 4
K_PASS = P * PACK
G = H // K_PASS
PAIRS = R // 2
QUADRANTS = 4
LAST = R - 1

G_TENSOR, G_VECTOR = 0, 1
SCALAR_ROUNDS = 2
PLANE_SPLIT = 4


def tile_linearrelationmeanjacobian_x2_kernel(
    tc, x, gin, w1, b1, gamma, w2_words, w2_scales, beta, out_0, out_1, out_2
):
    nc = tc.nc
    with ExitStack() as ctx:
        keep = ctx.enter_context(tc.tile_pool(name="keep", bufs=1))
        work = ctx.enter_context(tc.tile_pool(name="work", bufs=2))
        psum = ctx.enter_context(tc.psum_pool(name="psum", bufs=2))
        ctx.enter_context(tc.manual_schedule())

        ident_f32 = keep.tile([P, P], F32, name="ident_f32")
        ident_bf = keep.tile([P, P], BF16, name="ident_bf")
        gin_bf = keep.tile([P, PACK], BF16, name="gin_bf")
        b1_bf = keep.tile([P, G, PACK], BF16, name="b1_bf")
        gamma_bf = keep.tile([P, G, PACK], BF16, name="gamma_bf")
        beta_bf = keep.tile([P, R], BF16, name="beta_bf")
        b1_half = keep.tile([P, G, PACK], F32, name="b1_half")
        b1_full = keep.tile([P, G, PACK], F32, name="b1_full")
        gamma_n = keep.tile([P, G, PACK], F32, name="gamma_n")
        out_gain = keep.tile([P, R, PACK], F32, name="out_gain")
        warm = keep.tile([P, 1], F32, name="warm")
        warm_out = keep.tile([P, 1], F32, name="warm_out")
        x_raw = [keep.tile([P, 2, D], BF16, name="x_raw%d" % q) for q in range(PAIRS)]
        w1_raw = [keep.tile([P, PACK, K_PASS], BF16, name="w1_raw%d" % g) for g in range(G)]
        w1_grouped = [keep.tile([P, PACK, P, PACK], BF16, name="w1_grouped%d" % g, align_bytes=64) for g in range(G)]
        w1_codes = [keep.tile([P, K_PASS], U32, name="w1_codes%d" % g, align_bytes=64) for g in range(G)]
        w1_scales = [keep.tile([P, K_PASS], U8, name="w1_scales%d" % g, align_bytes=64) for g in range(G)]
        w1_t = [keep.tile([P, PACK, D], BF16, name="w1_t%d" % g) for g in range(G)]
        w2_codes = keep.tile([P, G, O], U32, name="w2_codes", align_bytes=64)
        w2_plane = keep.tile([P, G, O], U8, name="w2_plane", align_bytes=64)
        x_codes = [keep.tile([P, 2 * N], U32, name="x_codes%d" % q, align_bytes=64) for q in range(PAIRS)]
        x_scales = [keep.tile([P, 2 * N], U8, name="x_scales%d" % q, align_bytes=64) for q in range(PAIRS)]
        tanh_sum = keep.tile([P, PAIRS, G, PACK, 2], F32, name="tanh_sum")
        prod_sum = keep.tile([P, PAIRS, G, PACK, 2], F32, name="prod_sum")
        slope_sum = keep.tile([P, PAIRS, G, PACK, 2], F32, name="slope_sum")
        out_plane = keep.tile([P, R * D], U8, name="out_plane", align_bytes=64)
        live = {}

        def copy(on_scalar, out, in_):
            if on_scalar:
                nc.scalar.copy(out=out, in_=in_)
            else:
                nc.vector.tensor_copy(out=out, in_=in_)

        def load_inputs():
            nc.sync.dma_start(out=gin_bf[:], in_=gin.rearrange("(p t) -> p t", t=PACK))
            nc.sync.dma_start(out=x_raw[0][:], in_=x[0:2].rearrange("r n d -> n r d"))
            nc.scalar.dma_start(out=b1_bf[:], in_=b1.rearrange("(g p t) -> p g t", g=G, t=PACK))
            nc.scalar.dma_start(out=gamma_bf[:], in_=gamma.rearrange("(g p t) -> p g t", g=G, t=PACK))
            for g in range(G):
                cols = w1[:, g * K_PASS : (g + 1) * K_PASS]
                nc.sync.dma_start(out=w1_raw[g][:], in_=cols.rearrange("(p j) h -> p j h", j=PACK))
            for q in range(1, PAIRS):
                nc.sync.dma_start(out=x_raw[q][:], in_=x[2 * q : 2 * q + 2].rearrange("r n d -> n r d"))
            nc.sync.dma_start(
                out=w2_codes[:].bitcast(I32),
                in_=w2_words.rearrange("g p n t -> p g (n t)").bitcast(I32),
            )
            nc.sync.dma_start(out=beta_bf[:], in_=beta.partition_broadcast(P))

        def set_up():
            make_identity(nc, ident_f32[:])
            nc.vector.memset(warm[:], 0.0)
            nc.scalar.activation(out=warm_out[:], in_=warm[:], func=ACT.Silu)
            make_identity(nc, ident_bf[:])
            nc.gpsimd.memset(w2_plane[:].bitcast(I32), 0)
            for quad in range(QUADRANTS):
                nc.sync.dma_start(
                    out=w2_plane[32 * quad : 32 * quad + 4].bitcast(I32),
                    in_=w2_scales[:, 4 * quad : 4 * quad + 4, :].rearrange("g q n -> q g n").bitcast(I32),
                )

        def hidden_constants():
            nc.scalar.activation(out=b1_half[:], in_=b1_bf[:], func=ACT.Copy, scale=0.5)
            nc.scalar.activation(out=b1_full[:], in_=b1_bf[:], func=ACT.Copy)
            nc.scalar.activation(out=gamma_n[:], in_=gamma_bf[:], func=ACT.Copy, scale=0.5 / N)

        def output_gain():
            nc.vector.tensor_tensor(
                out=out_gain[:],
                in0=beta_bf[:].unsqueeze(2).to_broadcast([P, R, PACK]),
                in1=gin_bf[:].unsqueeze(1).to_broadcast([P, R, PACK]),
                op=ALU.mult,
            )


        def x_transpose(q):
            bank = psum.tile([P, 2, 2, N], F32, name="x_bank", tag="turn")
            pairs = x_raw[q][:].bitcast(F32)
            for i in range(2):
                for u in range(2):
                    nc.tensor.transpose(bank[:, u, i, :], pairs[:, i, u : D // 2 : 2], ident_f32[:])
            live["x_bank", q] = bank

        def x_gain(q):
            xg = work.tile([P, 2 * N, 2, 2], BF16, name="xg", align_bytes=64)
            src = live["x_bank", q][:].rearrange("p u i n -> p (u i n)").bitcast(BF16)
            nc.vector.tensor_tensor(
                out=xg[:],
                in0=src.rearrange("p (u m e) -> p m u e", u=2, e=2),
                in1=gin_bf[:].rearrange("p (u e) -> p u e", u=2).unsqueeze(1).to_broadcast([P, 2 * N, 2, 2]),
                op=ALU.mult,
            )
            live["xg", q] = xg

        def x_quantize(q):
            nc.vector.quantize_mx(
                out=x_codes[q][:].bitcast(FP8X4),
                scales=x_scales[q][:],
                in_=live["xg", q][:].rearrange("p m u e -> p (m u e)"),
            )

        def w1_interleave(g, half, on_scalar):
            ts = slice(2 * half, 2 * half + 2)
            copy(on_scalar, w1_grouped[g][:, ts], w1_raw[g][:].rearrange("p j (m t) -> p t m j", t=PACK)[:, ts])

        def w1_quantize(g, t0, t1):
            nc.vector.quantize_mx(
                out=w1_codes[g][:, t0 * P : t1 * P].bitcast(FP8X4),
                scales=w1_scales[g][:, t0 * P : t1 * P],
                in_=w1_grouped[g][:, t0:t1].rearrange("p t m j -> p (t m j)"),
            )

        def w1_transpose(g, half):
            bank = psum.tile([P, 2, PACK, P], BF16, name="w1_bank", tag="weave")
            for tl in range(2):
                for j in range(PACK):
                    src = w1_raw[g][:, j, 2 * half + tl : K_PASS : PACK]
                    nc.tensor.transpose(bank[:, tl, j, :], src, ident_bf[:])
            live["w1_bank", g, half] = bank

        def w1_copy_out(g, half, on_scalar):
            dst = w1_t[g][:, 2 * half : 2 * half + 2].rearrange("p t d -> p (t d)")
            copy(on_scalar, dst, live["w1_bank", g, half][:].rearrange("p t j c -> p (t j c)"))


        def hidden_matmul(s, half):
            q, g = divmod(s, G)
            bank = psum.tile([P, 2, 2 * N], F32, name="pre_bank", tag="pre")
            for tl in range(2):
                cols = slice((2 * half + tl) * P, (2 * half + tl + 1) * P)
                nc.tensor.matmul_mx(
                    out=bank[:, tl, :],
                    lhsT=w1_codes[g][:, cols].bitcast(FP8X4),
                    lhsT_scale=w1_scales[g][:, cols],
                    rhs=x_codes[q][:].bitcast(FP8X4),
                    rhs_scale=x_scales[q][:],
                    start=True,
                    stop=True,
                )
            live["pre", s, half] = bank

        def hidden_activations(s, half):
            q, g = divmod(s, G)
            bank = live["pre", s, half]
            silu = work.tile([P, 2, 2, N], F32, name="silu", bufs=4)
            tanh = work.tile([P, 2, 2, N], F32, name="tanh", bufs=4)
            for tl in range(2):
                t = 2 * half + tl
                nc.scalar.activation(
                    out=silu[:, tl].rearrange("p i n -> p (i n)"),
                    in_=bank[:, tl, :],
                    func=ACT.Silu,
                    bias=b1_full[:, g, t : t + 1],
                )
                for i in range(2):
                    nc.scalar.activation(
                        out=tanh[:, tl, i, :],
                        in_=bank[:, tl, i * N : (i + 1) * N],
                        func=ACT.Tanh,
                        bias=b1_half[:, g, t : t + 1],
                        scale=0.5,
                        accum_out=tanh_sum[:, q, g, t, i : i + 1],
                    )
            live["act", s, half] = (silu, tanh)

        def slope_products(s, half):
            q, g = divmod(s, G)
            silu, tanh = live["act", s, half]
            prod = work.tile([P, 2, 2, N], F32, name="prod", bufs=2 * G * PAIRS)
            for tl in (1, 0):
                for i in (1, 0):
                    nc.vector.scalar_tensor_tensor(
                        out=prod[:, tl, i, :],
                        in0=tanh[:, tl, i, :],
                        scalar=1.0,
                        in1=silu[:, tl, i, :],
                        op0=ALU.subtract,
                        op1=ALU.mult,
                        accum_out=prod_sum[:, q, g, 2 * half + tl, i : i + 1],
                    )

        def slope_sums(q):
            nc.vector.scalar_tensor_tensor(
                out=slope_sum[:, q].rearrange("p g t i -> p (g t i)"),
                in0=tanh_sum[:, q].rearrange("p g t i -> p (g t i)"),
                scalar=float(N),
                in1=prod_sum[:, q].rearrange("p g t i -> p (g t i)"),
                op0=ALU.add,
                op1=ALU.subtract,
            )


        def p_scale(r, g):
            rows = work.tile([P, PACK, D], BF16, name="p_rows", bufs=3)
            for t in range(PACK):
                nc.vector.tensor_scalar(
                    out=rows[:, t, :],
                    in0=w1_t[g][:, t, :],
                    scalar1=slope_sum[:, r // 2, g, t, r % 2 : r % 2 + 1],
                    scalar2=gamma_n[:, g, t : t + 1],
                    op0=ALU.mult,
                    op1=ALU.mult,
                )
            live["rows", r, g] = rows

        def p_grouped(r):
            if ("grouped", r) not in live:
                live["grouped", r] = work.tile([P, G, D, PACK], BF16, name="p_grouped", bufs=3, align_bytes=64)
            return live["grouped", r]

        def p_interleave_vector(r):
            nc.vector.tensor_copy(
                out=p_grouped(r)[:, G_VECTOR].rearrange("p (c i) t -> p c t i", i=4),
                in_=live["rows", r, G_VECTOR][:].rearrange("p t (c i) -> p c t i", i=4),
            )

        def p_interleave_tensor(r, half):
            bank = psum.tile([P, 2, P, PACK], BF16, name="weave_bank", tag="weave")
            for part in range(2):
                d0 = (2 * half + part) * P
                nc.tensor.matmul(
                    bank[:, part].rearrange("p d t -> p (d t)"),
                    lhsT=ident_bf[:],
                    rhs=live["rows", r, G_TENSOR][:, :, d0 : d0 + P].rearrange("p t d -> p d t"),
                    start=True,
                    stop=True,
                )
            live["weave", r, half] = bank

        def p_copy_out(r, half):
            cols = slice(half * D // 2, (half + 1) * D // 2)
            nc.scalar.copy(
                out=p_grouped(r)[:, G_TENSOR, cols, :].rearrange("p d t -> p (d t)"),
                in_=live["weave", r, half][:].rearrange("p s d t -> p (s d t)"),
            )

        def p_quantize(r):
            codes = work.tile([P, G, D], U32, name="p_codes", bufs=3, align_bytes=64)
            scales = work.tile([P, G, D], U8, name="p_scales", bufs=3, align_bytes=64)
            nc.vector.quantize_mx(
                out=codes[:].rearrange("p g d -> p (g d)").bitcast(FP8X4),
                scales=scales[:].rearrange("p g d -> p (g d)"),
                in_=p_grouped(r)[:].rearrange("p g d t -> p (g d t)"),
            )
            live["p", r] = (codes, scales)


        def out_matmul(r, j):
            bank = psum.tile([P, O], F32, name="k_bank", tag="weave" if r == LAST and j >= 2 else "k")
            cols = slice(j * P, (j + 1) * P)
            codes, scales = live["p", r]
            for g in range(G):
                nc.tensor.matmul_mx(
                    out=bank[:],
                    lhsT=codes[:, g, cols].bitcast(FP8X4),
                    lhsT_scale=scales[:, g, cols],
                    rhs=w2_codes[:, g, :].bitcast(FP8X4),
                    rhs_scale=w2_plane[:, g, :],
                    start=(g == 0),
                    stop=(g == G - 1),
                )
            live["k", r, j] = bank

        def y_copy_out(r, j):
            if ("y", r) not in live:
                live["y", r] = work.tile([P, PACK, O], F32, name="y", bufs=4)
            nc.scalar.activation(
                out=live["y", r][:, j, :], in_=live["k", r, j][:], func=ACT.Copy, scale=out_gain[:, r, j : j + 1]
            )

        def y_store(r, half):
            js = slice(2 * half, 2 * half + 2)
            rows = out_0[r].rearrange("(c j) o -> c j o", j=PACK)
            nc.sync.dma_start(out=rows[:, js, :], in_=live["y", r][:, js, :])

        def y_round(r, j0, j1, on_scalar):
            if ("y_bf", r) not in live:
                live["y_bf", r] = work.tile([P, PACK, O], BF16, name="y_bf", bufs=3)
            dst = live["y_bf", r][:, j0:j1, :].rearrange("p j (u m e) -> p j u m e", u=2, e=2)
            src = live["y", r][:, j0:j1, :].rearrange("p j (m u e) -> p j u m e", u=2, e=2)
            copy(on_scalar, dst, src)

        def y_round_vector(r):
            y_round(r, 2 if r < SCALAR_ROUNDS else 0, PACK, False)

        def y_transpose(r, half):
            bank = psum.tile([P, 2, 2, P], F32, name="y_bank", tag="turn")
            pairs = live["y_bf", r][:, 2 * half : 2 * half + 2, :].bitcast(F32)
            for jl in range(2):
                for u in range(2):
                    nc.tensor.transpose(bank[:, jl, u, :], pairs[:, jl, u * P : (u + 1) * P], ident_f32[:])
            live["y_bank", r, half] = bank

        def y_interleave(r, half):
            if ("y_grouped", r) not in live:
                live["y_grouped", r] = work.tile([P, P, PACK, 2], F32, name="y_grouped", bufs=3, align_bytes=64)
            nc.scalar.copy(
                out=live["y_grouped", r][:, :, 2 * half : 2 * half + 2, :],
                in_=live["y_bank", r, half][:].rearrange("p j u c -> p c j u"),
            )

        def y_quantize(r):
            codes = work.tile([P, D], U32, name="y_codes", bufs=R, align_bytes=64)
            cols = slice(r * D, (r + 1) * D)
            nc.vector.quantize_mx(
                out=codes[:].bitcast(FP8X4),
                scales=out_plane[:, cols],
                in_=live["y_grouped", r][:].rearrange("p c j u -> p (c j u)").bitcast(BF16),
            )
            nc.sync.dma_start(
                out=out_1[0, :, cols, :].rearrange("p m t -> p (m t)").bitcast(I32), in_=codes[:].bitcast(I32)
            )

        def scale_rows_store(queue, r0, r1):
            cols = slice(r0 * D, r1 * D)
            for quad in range(QUADRANTS):
                queue.dma_start(
                    out=out_2[0, 4 * quad : 4 * quad + 4, cols].bitcast(I32),
                    in_=out_plane[32 * quad : 32 * quad + 4, cols].bitcast(I32),
                )

        load_inputs()
        set_up()
        x_transpose(0)
        w1_interleave(0, 1, True)
        w1_transpose(0, 1)
        x_gain(0)
        w1_interleave(1, 0, True)
        w1_interleave(0, 0, False)
        w1_quantize(0, 0, 2)
        w1_quantize(0, 2, PACK)
        w1_transpose(1, 1)
        hidden_constants()
        w1_interleave(1, 1, False)
        x_quantize(0)
        w1_quantize(1, 0, PACK)
        x_transpose(1)
        x_gain(1)
        x_quantize(1)
        w1_copy_out(1, 1, True)

        units = range(G * PAIRS)
        relations = range(R)
        steady = range(LAST)
        once = (0,)
        last = (LAST,)
        timetable = [
            (5, relations, lambda r: p_copy_out(r, 0)),
            (6, steady, lambda r: y_copy_out(r, 2)),
            (6, last, lambda r: y_copy_out(r, 3)),
            (4, relations, lambda r: p_scale(r, G_TENSOR)),
            (5, relations, p_interleave_vector),
            (-3, units[2 * G :: G], lambda s: x_gain(s // G)),
            (1, units, lambda s: hidden_activations(s, 1)),
            (9, steady, lambda r: y_interleave(r, 1)),
            (9, steady, lambda r: y_transpose(r, 0)),
            (2, once, lambda i: w1_copy_out(0, 0, False)),
            (2, units, lambda s: slope_products(s, 1)),
            (4, relations, lambda r: p_interleave_tensor(r, 1)),
            (5, once, lambda i: output_gain()),
            (6, steady, lambda r: out_matmul(r, 3)),
            (6, steady, lambda r: out_matmul(r, 0)),
            (7, last, lambda r: out_matmul(r, 1)),
            (0, once, lambda i: w1_copy_out(0, 1, True)),
            (11, range(LAST - 2), y_quantize),
            (11 + PLANE_SPLIT - 1, once, lambda i: scale_rows_store(nc.sync, 0, PLANE_SPLIT)),
            (-3, units[2 * G :: G], lambda s: x_quantize(s // G)),
            (5, relations, p_quantize),
            (0, units, lambda s: hidden_matmul(s, 0)),
            (4, relations, lambda r: p_scale(r, G_VECTOR)),
            (5, last, lambda r: out_matmul(r, 2)),
            (6, steady, lambda r: y_copy_out(r, 3)),
            (4, relations, lambda r: p_interleave_tensor(r, 0)),
            (-4, units[2 * G :: G], lambda s: x_transpose(s // G)),
            (9, steady, lambda r: y_interleave(r, 0)),
            (6, steady, lambda r: y_copy_out(r, 0)),
            (5, last, lambda r: out_matmul(r, 3)),
            (5, last, lambda r: y_copy_out(r, 2)),
            (2, units[1::G], lambda s: slope_sums(s // G)),
            (6, last, lambda r: y_store(r, 1)),
            (1, once, lambda i: w1_transpose(1, 0)),
            (0, units, lambda s: hidden_activations(s, 0)),
            (6, steady, lambda r: y_store(r, 1)),
            (5, steady, lambda r: out_matmul(r, 1)),
            (0, units, lambda s: hidden_matmul(s, 1)),
            (8, steady, y_round_vector),
            (0, once, lambda i: w1_transpose(0, 0)),
            (6, last, lambda r: out_matmul(r, 0)),
            (5, steady, lambda r: out_matmul(r, 2)),
            (8, range(SCALAR_ROUNDS), lambda r: y_round(r, 0, 2, True)),
            (6, steady, lambda r: y_store(r, 0)),
            (8, steady, lambda r: y_transpose(r, 1)),
            (6, last, lambda r: y_copy_out(r, 0)),
            (7, last, lambda r: y_copy_out(r, 1)),
            (2, once, lambda i: w1_copy_out(1, 0, False)),
            (4, relations, lambda r: p_copy_out(r, 1)),
            (1, units, lambda s: slope_products(s, 0)),
            (5, steady, lambda r: y_copy_out(r, 1)),
        ]
        for slot in range(2 * R):
            for first, indices, step in timetable:
                if slot - first in indices:
                    step(slot - first)

        y_store(LAST, 0)
        y_round(LAST, 2, PACK, False)
        y_quantize(LAST - 2)
        y_round(LAST, 0, 2, False)
        y_quantize(LAST - 1)
        for half in (1, 0):
            y_transpose(LAST, half)
            y_interleave(LAST, half)
        y_quantize(LAST)
        scale_rows_store(nc.scalar, PLANE_SPLIT, R)
